import numpy as np
import ml_dtypes


def mxq(x, axis, fmt="e4m3"):
    dtype, down = {"e4m3": (ml_dtypes.float8_e4m3fn, 7), "e5m2": (ml_dtypes.float8_e5m2, 14)}[fmt]
    v = np.moveaxis(np.asarray(x, np.float32).astype(ml_dtypes.bfloat16).astype(np.float64), axis, -1)
    blocks = v.reshape(v.shape[:-1] + (-1, 32))
    amax = np.abs(blocks).max(-1, keepdims=True)
    byte = np.maximum(np.where(amax > 0, np.frexp(amax)[1] - 1 + 127, 0) - down, 1)
    scale = np.exp2(byte - 127.0)
    codes = (blocks / scale).astype(np.float32).astype(dtype).astype(np.float64)
    return np.moveaxis((codes * scale).reshape(v.shape), -1, axis)


WIDE = False


def mx_kscale(k):
    if not WIDE:
        return np.ones(k)
    levels = np.array([10, -10, 5, -5, 0])
    if k % 512:
        return np.exp2(np.random.permutation(np.resize(levels, k // 32))).repeat(32)
    a = np.empty((k // 512, 16))
    for p in range(k // 512):
        a[p, :8] = np.random.permutation(np.resize(levels, 8))
        for g in range(8):
            far = levels[np.abs(levels - a[p, g]) >= 10]
            a[p, g + 8] = far[np.random.randint(len(far))]
    return np.exp2(a.ravel()).repeat(32)


BF16 = ml_dtypes.bfloat16


def bf(x):
    return np.asarray(x, np.float32).astype(BF16)


def f64(x):
    return np.asarray(x).astype(np.float64)

def planes(Y):
    n, m = Y.shape
    b = f64(bf(Y)).reshape(n // 32, 32, m)
    amax = np.abs(b).max(1)
    byte = np.clip(np.where(amax > 0, np.frexp(amax)[1] - 1 + 127 - 7, 1), 1, 254)
    codes = (b * np.exp2(127.0 - byte)[:, None, :]).reshape(n, m).astype(np.float32).astype(ml_dtypes.float8_e4m3fn).view(np.uint8)
    words = codes.reshape(n // 512, 128, 4, m).transpose(0, 1, 3, 2)
    return np.ascontiguousarray(words), np.ascontiguousarray(byte.astype(np.uint8).reshape(n // 512, 16, m))


B, S, H, P, N = 1, 1024, 4, 128, 512


def event_decay(age, lam):
    age_t = age[:, :, None]
    age_s = age[:, None, :]
    gap = np.maximum(age_t - age_s, 0.0)
    keep = age_t >= age_s
    decay = np.exp(-lam[None, :, None, None] * gap[:, None, :, :])
    return np.where(keep[:, None, :, :], decay, 0.0)


def setup_inputs():
    s = mx_kscale(N)
    t = mx_kscale(S)
    return {
        "cm": bf(np.random.standard_normal((B, S, N)) / np.sqrt(N) * s),
        "bm": bf(np.random.standard_normal((B, S, N)) / s[None, None, :] * t[None, :, None]),
        "v": bf(np.random.standard_normal((B, H, S, P)) * 3.2 / np.sqrt(S) / t[None, None, :, None]),
        "dt": bf(np.random.uniform(0.5, 1.5, (B, H, S))),
        "age": bf(np.random.uniform(0.0, 2.0, (B, S))),
        "lam": bf(np.random.uniform(0.5, 1.5, (H,))),
        "h0": bf(np.random.standard_normal((B, H, N, P)) * 2.0 / s[None, None, :, None]),
    }


def core(cm, bm, v, dt, age, lam, h0):
    age, lam = f64(age), f64(lam)
    cq = mxq(f64(cm), 2, "e4m3")
    g = cq @ mxq(f64(bm), 2, "e4m3").transpose(0, 2, 1)
    l = event_decay(age, lam)
    m = g[:, None, :, :] * l
    w = f64(dt)[:, :, :, None] * f64(v)
    yi = mxq(m, 3, "e4m3") @ mxq(w, 2, "e4m3")
    r = cq[:, None, :, :] @ mxq(f64(h0), 2, "e4m3")
    carry = np.exp(-lam[None, :, None] * age[:, None, :])
    return yi + carry[:, :, :, None] * r


def reference(cm, bm, v, dt, age, lam, h0):
    R_out = core(cm, bm, v, dt, age, lam, h0)
    words, scales = planes(np.moveaxis(R_out, 2, 0).reshape(1024, -1))
    return R_out, words, scales

@@ -1,0 +1,277 @@
+from contextlib import ExitStack
+
+import concourse.mybir as mybir
+from concourse.masks import make_identity
+
+S, H, W, N = 1024, 4, 128, 512
+FLOPS = 2 * S * S * N + 2 * H * S * S * W + 2 * H * S * N * W
+
+F32 = mybir.dt.float32
+BF16 = mybir.dt.bfloat16
+U32 = mybir.dt.uint32
+I32 = mybir.dt.int32
+U8 = mybir.dt.uint8
+FP8X4 = mybir.dt.float8_e4m3fn_x4
+ALU = mybir.AluOpType
+ACT = mybir.ActivationFunctionType
+
+P = 128
+PACK = 4
+GROUP = P * PACK
+GROUPS = S // GROUP
+RUN = 4
+
+
+def tile_eventtimestatespacedualchunk_x1_kernel(tc, cm, bm, v, dt, age, lam, h0, out_0, out_1, out_2):
+    nc = tc.nc
+    with ExitStack() as ctx:
+        keep = ctx.enter_context(tc.tile_pool(name="keep", bufs=1))
+        flow = ctx.enter_context(tc.tile_pool(name="flow", bufs=2))
+        psum = ctx.enter_context(tc.psum_pool(name="psum", bufs=2))
+        ctx.enter_context(tc.manual_schedule())
+
+        def operand(name, width):
+            codes = keep.tile([P, width], U32, name=name + "_codes", align_bytes=64)
+            scales = keep.tile([P, width], U8, name=name + "_scales", align_bytes=64)
+            return codes, scales
+
+        def quantize(codes, scales, values):
+            nc.vector.quantize_mx(out=codes.bitcast(FP8X4), scales=scales, in_=values)
+
+        def multiply(acc, lhs, lhs_cols, rhs, rhs_cols, start, stop):
+            nc.tensor.matmul_mx(
+                out=acc,
+                lhsT=lhs[0][:, lhs_cols].bitcast(FP8X4), lhsT_scale=lhs[1][:, lhs_cols],
+                rhs=rhs[0][:, rhs_cols].bitcast(FP8X4), rhs_scale=rhs[1][:, rhs_cols],
+                start=start, stop=stop,
+            )
+
+        def block(i, width=P):
+            return slice(i * width, (i + 1) * width)
+
+        def rows_view(ap):
+            return ap.rearrange("p j (c i) -> p c j i", i=RUN)
+
+        def packed_view(ap):
+            return ap.rearrange("p (c i j) -> p c j i", i=RUN, j=PACK)
+
+        age_col = keep.tile([P, GROUPS, PACK], BF16)
+        nc.sync.dma_start(out=age_col[:], in_=age[0].rearrange("(g p j) -> p g j", p=P, j=PACK))
+        lam_all = keep.tile([P, H], BF16)
+        nc.sync.dma_start(out=lam_all[:], in_=lam.partition_broadcast(P))
+
+        def load_rows(name, x, g):
+            raw = keep.tile([P, PACK, N], BF16, name=name)
+            nc.sync.dma_start(out=raw[:], in_=x[0, block(g, GROUP), :].rearrange("(p j) n -> p j n", j=PACK))
+            return raw
+
+        cm_raw = [load_rows("cm_raw0", cm, 0)]
+        bm_raw = [load_rows("bm_raw0", bm, 0), load_rows("bm_raw1", bm, 1)]
+        dt_col = keep.tile([P, H * GROUPS, PACK], BF16)
+        nc.sync.dma_start(out=dt_col[:], in_=dt[0].rearrange("h (g p j) -> p (h g) j", p=P, j=PACK))
+        v_raw = keep.tile([P, H * GROUPS, PACK * W], BF16)
+        nc.sync.dma_start(out=v_raw[:], in_=v[0].rearrange("h (g p j) w -> p (h g) (j w)", p=P, j=PACK))
+        h0_raw = keep.tile([P, H, PACK * W], BF16)
+        nc.sync.dma_start(out=h0_raw[:], in_=h0[0].rearrange("h (p j) w -> p h (j w)", j=PACK))
+        cm_raw.append(load_rows("cm_raw1", cm, 1))
+
+        ident_bf = keep.tile([P, P], BF16)
+        make_identity(nc, ident_bf[:])
+        ident_f32 = keep.tile([P, P], F32)
+        make_identity(nc, ident_f32[:])
+
+        age_flat = age_col[:].rearrange("p g j -> p (g j)")
+        lam_age = keep.tile([P, H, GROUPS * PACK], F32)
+        nc.vector.tensor_tensor(
+            out=lam_age[:],
+            in0=age_flat.unsqueeze(1).to_broadcast([P, H, GROUPS * PACK]),
+            in1=lam_all[:].unsqueeze(2).to_broadcast([P, H, GROUPS * PACK]),
+            op=ALU.mult,
+        )
+        neg_lam = keep.tile([P, H], F32)
+        nc.vector.tensor_scalar(out=neg_lam[:], in0=lam_all[:], scalar1=-1.0, scalar2=None, op0=ALU.mult)
+        carry = keep.tile([P, H, GROUPS * PACK], F32)
+        nc.scalar.activation(out=carry[:], in_=lam_age[:], func=ACT.Exp, scale=-1.0)
+
+        spread = psum.tile([P, S], BF16, tag="turn", bufs=3)
+        for k in range(GROUPS * PACK):
+            nc.tensor.matmul(spread[:, block(k)], lhsT=age_flat[:, k:k + 1].to_broadcast([P, P]), rhs=ident_bf[:],
+                             start=True, stop=True)
+        age_row = keep.tile([P, S], BF16)
+        nc.vector.tensor_copy(out=age_row[:], in_=spread[:])
+        later = keep.tile([P, GROUPS * PACK, S], BF16)
+        for k in range(GROUPS * PACK):
+            nc.vector.tensor_scalar(out=later[:, k, :], in0=age_row[:], scalar1=age_flat[:, k:k + 1], scalar2=None,
+                                    op0=ALU.max)
+
+        cq = [operand("cq%d" % g, GROUP) for g in range(GROUPS)]
+        bq = [operand("bq%d" % g, GROUP) for g in range(GROUPS)]
+        wq = [operand("wq%d" % h, GROUPS * W) for h in range(H)]
+        hq = operand("hq", H * W)
+        oq = [operand("oq%d" % g, H * W) for g in range(GROUPS)]
+        masked = [[keep.tile([P, PACK, GROUP], F32, name="masked%d%d" % (tg, g)) for g in range(GROUPS)]
+                  for tg in range(GROUPS)]
+        read = [keep.tile([P, H, PACK, W], F32, name="read%d" % tg) for tg in range(GROUPS)]
+
+        def turn(raw):
+            words = raw[:].rearrange("p j n -> p (j n)").bitcast(F32)
+            turned = flow.tile([P, GROUP * PACK], BF16, tag="turned", bufs=2, align_bytes=64)
+            turned_words = turned[:].bitcast(F32)
+            banks = []
+            for b in range(2):
+                bank = psum.tile([P, 2, 2, P], F32, tag="turn", bufs=3)
+                for jj in range(2):
+                    j = 2 * b + jj
+                    for u in range(2):
+                        nc.tensor.transpose(bank[:, jj, u, :], words[:, 256 * j + u:256 * (j + 1):2], ident_f32[:])
+                banks.append(bank)
+            for b in range(2):
+                nc.scalar.copy(out=turned_words[:, block(b, GROUP)].rearrange("p (jj m u) -> p jj m u", jj=2, u=2),
+                               in_=banks[b][:].rearrange("p jj u m -> p jj m u"))
+            return turned
+
+        def scores(tg, g, slots):
+            for j in slots:
+                bank = psum.tile([P, GROUP], F32, tag="score", bufs=2)
+                multiply(bank[:], bq[g], block(j), cq[tg], slice(0, GROUP), True, True)
+                k = g * PACK + j
+                nc.vector.scalar_tensor_tensor(
+                    out=masked[tg][g][:, j, :], in0=age_row[:, block(tg, GROUP)], scalar=age_flat[:, k:k + 1],
+                    in1=bank[:], op0=ALU.is_ge, op1=ALU.mult)
+
+        w_bf = {}
+
+        def scale_values(h):
+            w_bf[h] = flow.tile([P, GROUPS, W * PACK], BF16, name="w_bf", tag="w_bf", bufs=2, align_bytes=64)
+            for g in range(GROUPS):
+                hg = h * GROUPS + g
+                nc.vector.tensor_tensor(
+                    out=packed_view(w_bf[h][:, g, :]),
+                    in0=rows_view(v_raw[:, hg, :].rearrange("p (j w) -> p j w", j=PACK)),
+                    in1=dt_col[:, hg, :].unsqueeze(1).unsqueeze(3).to_broadcast([P, W // RUN, PACK, RUN]),
+                    op=ALU.mult)
+
+        def quantize_values(h):
+            quantize(wq[h][0][:], wq[h][1][:], w_bf[h][:].rearrange("p g x -> p (g x)"))
+
+        def pack_state():
+            h0_bf = keep.tile([P, H, W * PACK], BF16, align_bytes=64)
+            for h in range(H):
+                nc.scalar.copy(out=packed_view(h0_bf[:, h, :]),
+                               in_=rows_view(h0_raw[:, h, :].rearrange("p (j w) -> p j w", j=PACK)))
+            return h0_bf
+
+        def read_state(tg):
+            for j in range(PACK):
+                bank = psum.tile([P, H * W], F32, tag="score", bufs=2)
+                multiply(bank[:], cq[tg], block(j), hq, slice(0, H * W), True, True)
+                k = tg * PACK + j
+                for h in range(H):
+                    nc.scalar.activation(out=read[tg][:, h, j, :], in_=bank[:, block(h)], func=ACT.Copy,
+                                         scale=carry[:, h, k:k + 1])
+
+        def step_of(k):
+            return k // (H * GROUPS), (k // GROUPS) % H, k % GROUPS
+
+        decay, m_bf, mq, inner, result, result_bf = {}, {}, {}, {}, {}, {}
+
+        def decays(k):
+            tg, h, g = step_of(k)
+            decay[k] = flow.tile([P, PACK, GROUP], F32, name="decay", tag="decay", bufs=4)
+            for j in range(PACK):
+                i = g * PACK + j
+                nc.scalar.activation(out=decay[k][:, j, :], in_=later[:, i, block(tg, GROUP)], func=ACT.Exp,
+                                     scale=neg_lam[:, h:h + 1], bias=lam_age[:, h, i:i + 1])
+
+        def decay_scores(k):
+            tg, h, g = step_of(k)
+            m_bf[k] = flow.tile([P, GROUP * PACK], BF16, name="m_bf", tag="m_bf", bufs=3, align_bytes=64)
+            nc.vector.tensor_tensor(out=packed_view(m_bf[k][:]), in0=rows_view(masked[tg][g][:]),
+                                    in1=rows_view(decay[k][:]), op=ALU.mult)
+
+        def quantize_scores(k):
+            codes = flow.tile([P, GROUP], U32, name="m_codes", tag="m_codes", bufs=4, align_bytes=64)
+            scales = flow.tile([P, GROUP], U8, name="m_scales", tag="m_scales", bufs=4, align_bytes=64)
+            mq[k] = (codes, scales)
+            quantize(codes[:], scales[:], m_bf[k][:])
+            if k % GROUPS == GROUPS - 1:
+                u = k // GROUPS
+                h = u % H
+                inner[u] = psum.tile([P, PACK, W], F32, name="inner", tag="inner", bufs=3)
+                for j in range(PACK):
+                    for g in range(GROUPS):
+                        multiply(inner[u][:, j, :], mq[u * GROUPS + g], block(j), wq[h], block(g), g == 0,
+                                 g == GROUPS - 1)
+
+        def finish(u):
+            tg, h = divmod(u, H)
+            result[u] = flow.tile([P, PACK, W], F32, name="result", tag="result", bufs=3)
+            nc.vector.tensor_tensor(out=result[u][:], in0=inner[u][:], in1=read[tg][:, h, :, :], op=ALU.add)
+            result_bf[u] = flow.tile([P, W * PACK], BF16, name="result_bf", tag="result_bf", bufs=2, align_bytes=64)
+            nc.scalar.copy(out=packed_view(result_bf[u][:]), in_=rows_view(result[u][:]))
+            nc.sync.dma_start(out=out_0[0, h, block(tg, GROUP), :].rearrange("(p j) w -> p j w", j=PACK),
+                              in_=result[u][:])
+
+        def quantize_result(u):
+            tg, h = divmod(u, H)
+            codes, scales = oq[tg]
+            quantize(codes[:, block(h)], scales[:, block(h)], result_bf[u][:])
+            nc.sync.dma_start(out=out_1[tg].rearrange("p m t -> p (m t)").bitcast(I32)[:, block(h)],
+                              in_=codes[:, block(h)].bitcast(I32))
+            if h == H - 1:
+                for q in range(4):
+                    nc.sync.dma_start(out=out_2[tg, 4 * q:4 * q + 4, :].bitcast(I32),
+                                      in_=scales[32 * q:32 * q + 4, :].bitcast(I32))
+
+        cm_turned = turn(cm_raw[0])
+        bm_turned = turn(bm_raw[0])
+        quantize(cq[0][0][:], cq[0][1][:], cm_turned[:])
+        quantize(bq[0][0][:], bq[0][1][:], bm_turned[:])
+        decays(0)
+        bm_turned = turn(bm_raw[1])
+        scores(0, 0, range(PACK))
+        decays(1)
+        h0_bf = pack_state()
+
+        steps = GROUPS * H * GROUPS
+        for k in range(steps):
+            decay_scores(k)
+            if k + 2 < steps:
+                decays(k + 2)
+            if k == 0:
+                quantize(bq[1][0][:], bq[1][1][:], bm_turned[:])
+                cm_turned = turn(cm_raw[1])
+                scale_values(0)
+                scores(0, 1, range(PACK))
+                quantize_values(0)
+            if k >= 1:
+                quantize_scores(k - 1)
+            if k == 1:
+                quantize(hq[0][:], hq[1][:], h0_bf[:].rearrange("p h x -> p (h x)"))
+                read_state(0)
+                scale_values(1)
+            if k == 2:
+                quantize(cq[1][0][:], cq[1][1][:], cm_turned[:])
+                quantize_values(1)
+            if k == 3:
+                scale_values(2)
+            if k == 4:
+                quantize_values(2)
+                scores(1, 0, range(0, 2))
+                scale_values(3)
+            if k == 5:
+                scores(1, 0, range(2, 4))
+            if k == 6:
+                quantize_values(3)
+                scores(1, 1, range(0, 2))
+            if k == 7:
+                scores(1, 1, range(2, 4))
+                read_state(1)
+            if k >= 3 and k % 2 == 1:
+                finish((k - 3) // 2)
+            if k >= 4 and k % 2 == 0:
+                quantize_result((k - 4) // 2)
+        quantize_scores(steps - 1)
+        quantize_result(GROUPS * H - 2)
+        finish(GROUPS * H - 1)
+        quantize_result(GROUPS * H - 1)

@@ -20,6 +20,8 @@ PACK = 4
 GROUP = P * PACK
 GROUPS = S // GROUP
 RUN = 4
+HELD = 3
+BANKS = {"held": 5, "score": 1, "inner": 2}
 
 
 def tile_eventtimestatespacedualchunk_x1_kernel(tc, cm, bm, v, dt, age, lam, h0, out_0, out_1, out_2):
@@ -57,23 +59,30 @@ def tile_eventtimestatespacedualchunk_x1_kernel(tc, cm, bm, v, dt, age, lam, h0,
 
         age_col = keep.tile([P, GROUPS, PACK], BF16)
         nc.sync.dma_start(out=age_col[:], in_=age[0].rearrange("(g p j) -> p g j", p=P, j=PACK))
-        lam_all = keep.tile([P, H], BF16)
-        nc.sync.dma_start(out=lam_all[:], in_=lam.partition_broadcast(P))
 
         def load_rows(name, x, g):
             raw = keep.tile([P, PACK, N], BF16, name=name)
             nc.sync.dma_start(out=raw[:], in_=x[0, block(g, GROUP), :].rearrange("(p j) n -> p j n", j=PACK))
             return raw
 
+        def load_values(h):
+            raw = keep.tile([P, GROUPS, PACK * W], BF16, name="v_raw%d" % h)
+            nc.sync.dma_start(out=raw[:], in_=v[0, h].rearrange("(g p j) w -> p g (j w)", p=P, j=PACK))
+            return raw
+
         cm_raw = [load_rows("cm_raw0", cm, 0)]
-        bm_raw = [load_rows("bm_raw0", bm, 0), load_rows("bm_raw1", bm, 1)]
+        lam_all = keep.tile([P, H], BF16)
+        nc.sync.dma_start(out=lam_all[:], in_=lam.partition_broadcast(P))
+        bm_raw = [load_rows("bm_raw0", bm, 0)]
         dt_col = keep.tile([P, H * GROUPS, PACK], BF16)
         nc.sync.dma_start(out=dt_col[:], in_=dt[0].rearrange("h (g p j) -> p (h g) j", p=P, j=PACK))
-        v_raw = keep.tile([P, H * GROUPS, PACK * W], BF16)
-        nc.sync.dma_start(out=v_raw[:], in_=v[0].rearrange("h (g p j) w -> p (h g) (j w)", p=P, j=PACK))
+        v_raw = [load_values(0)]
+        bm_raw.append(load_rows("bm_raw1", bm, 1))
         h0_raw = keep.tile([P, H, PACK * W], BF16)
         nc.sync.dma_start(out=h0_raw[:], in_=h0[0].rearrange("h (p j) w -> p h (j w)", j=PACK))
         cm_raw.append(load_rows("cm_raw1", cm, 1))
+        for h in range(1, H):
+            v_raw.append(load_values(h))
 
         ident_bf = keep.tile([P, P], BF16)
         make_identity(nc, ident_bf[:])
@@ -81,6 +90,12 @@ def tile_eventtimestatespacedualchunk_x1_kernel(tc, cm, bm, v, dt, age, lam, h0,
         make_identity(nc, ident_f32[:])
 
         age_flat = age_col[:].rearrange("p g j -> p (g j)")
+        spread = psum.tile([P, S], BF16, tag="held", bufs=BANKS["held"])
+        for k in range(GROUPS * PACK):
+            nc.tensor.matmul(spread[:, block(k)], lhsT=age_flat[:, k:k + 1].to_broadcast([P, P]), rhs=ident_bf[:],
+                             start=True, stop=True)
+        age_row = keep.tile([P, S], BF16)
+        nc.vector.tensor_copy(out=age_row[:], in_=spread[:])
         lam_age = keep.tile([P, H, GROUPS * PACK], F32)
         nc.vector.tensor_tensor(
             out=lam_age[:],
@@ -93,12 +108,6 @@ def tile_eventtimestatespacedualchunk_x1_kernel(tc, cm, bm, v, dt, age, lam, h0,
         carry = keep.tile([P, H, GROUPS * PACK], F32)
         nc.scalar.activation(out=carry[:], in_=lam_age[:], func=ACT.Exp, scale=-1.0)
 
-        spread = psum.tile([P, S], BF16, tag="turn", bufs=3)
-        for k in range(GROUPS * PACK):
-            nc.tensor.matmul(spread[:, block(k)], lhsT=age_flat[:, k:k + 1].to_broadcast([P, P]), rhs=ident_bf[:],
-                             start=True, stop=True)
-        age_row = keep.tile([P, S], BF16)
-        nc.vector.tensor_copy(out=age_row[:], in_=spread[:])
         later = keep.tile([P, GROUPS * PACK, S], BF16)
         for k in range(GROUPS * PACK):
             nc.vector.tensor_scalar(out=later[:, k, :], in0=age_row[:], scalar1=age_flat[:, k:k + 1], scalar2=None,
@@ -109,17 +118,15 @@ def tile_eventtimestatespacedualchunk_x1_kernel(tc, cm, bm, v, dt, age, lam, h0,
         wq = [operand("wq%d" % h, GROUPS * W) for h in range(H)]
         hq = operand("hq", H * W)
         oq = [operand("oq%d" % g, H * W) for g in range(GROUPS)]
-        masked = [[keep.tile([P, PACK, GROUP], F32, name="masked%d%d" % (tg, g)) for g in range(GROUPS)]
-                  for tg in range(GROUPS)]
         read = [keep.tile([P, H, PACK, W], F32, name="read%d" % tg) for tg in range(GROUPS)]
 
-        def turn(raw):
+        def turn(raw, tag):
             words = raw[:].rearrange("p j n -> p (j n)").bitcast(F32)
             turned = flow.tile([P, GROUP * PACK], BF16, tag="turned", bufs=2, align_bytes=64)
             turned_words = turned[:].bitcast(F32)
             banks = []
             for b in range(2):
-                bank = psum.tile([P, 2, 2, P], F32, tag="turn", bufs=3)
+                bank = psum.tile([P, 2, 2, P], F32, tag=tag, bufs=BANKS[tag])
                 for jj in range(2):
                     j = 2 * b + jj
                     for u in range(2):
@@ -130,14 +137,42 @@ def tile_eventtimestatespacedualchunk_x1_kernel(tc, cm, bm, v, dt, age, lam, h0,
                                in_=banks[b][:].rearrange("p jj u m -> p jj m u"))
             return turned
 
-        def scores(tg, g, slots):
-            for j in slots:
-                bank = psum.tile([P, GROUP], F32, tag="score", bufs=2)
-                multiply(bank[:], bq[g], block(j), cq[tg], slice(0, GROUP), True, True)
-                k = g * PACK + j
+        score, flipped, masked = {}, {}, {}
+
+        def scores(group, tile_j, tag):
+            tg, g = divmod(group, GROUPS)
+            bank = psum.tile([P, PACK, P], F32, name="score", tag=tag, bufs=BANKS[tag])
+            score[group, tile_j] = bank
+            if tile_j < HELD:
+                multiply(bank[:].rearrange("p j m -> p (j m)"), cq[tg], block(tile_j), bq[g], slice(0, GROUP), True, True)
+            else:
+                for j in range(PACK):
+                    multiply(bank[:, j, :], bq[g], block(j), cq[tg], block(tile_j), True, True)
+
+        def mask_scores(group, tile_j):
+            tg, g = divmod(group, GROUPS)
+            bank = score[group, tile_j]
+            if tile_j < HELD:
+                k = tg * PACK + tile_j
+                kept = flow.tile([P, GROUP], F32, name="flipped", tag="flipped", bufs=3)
                 nc.vector.scalar_tensor_tensor(
-                    out=masked[tg][g][:, j, :], in0=age_row[:, block(tg, GROUP)], scalar=age_flat[:, k:k + 1],
-                    in1=bank[:], op0=ALU.is_ge, op1=ALU.mult)
+                    out=kept[:], in0=age_row[:, block(g, GROUP)], scalar=age_flat[:, k:k + 1],
+                    in1=bank[:].rearrange("p j m -> p (j m)"), op0=ALU.is_le, op1=ALU.mult)
+                flipped[group, tile_j] = kept
+            else:
+                kept = flow.tile([P, PACK, P], F32, name="direct", tag="direct", bufs=2)
+                for j in range(PACK):
+                    k = g * PACK + j
+                    nc.vector.scalar_tensor_tensor(
+                        out=kept[:, j, :], in0=age_row[:, block(tg * PACK + tile_j)], scalar=age_flat[:, k:k + 1],
+                        in1=bank[:, j, :], op0=ALU.is_ge, op1=ALU.mult)
+                masked[group, tile_j] = kept
+
+        def hold_scores(group, tile_j):
+            bank = psum.tile([P, PACK, P], F32, name="held", tag="held", bufs=BANKS["held"])
+            for j in range(PACK):
+                nc.tensor.transpose(bank[:, j, :], flipped[group, tile_j][:, block(j)], ident_f32[:])
+            masked[group, tile_j] = bank
 
         w_bf = {}
 
@@ -147,7 +182,7 @@ def tile_eventtimestatespacedualchunk_x1_kernel(tc, cm, bm, v, dt, age, lam, h0,
                 hg = h * GROUPS + g
                 nc.vector.tensor_tensor(
                     out=packed_view(w_bf[h][:, g, :]),
-                    in0=rows_view(v_raw[:, hg, :].rearrange("p (j w) -> p j w", j=PACK)),
+                    in0=rows_view(v_raw[h][:, g, :].rearrange("p (j w) -> p j w", j=PACK)),
                     in1=dt_col[:, hg, :].unsqueeze(1).unsqueeze(3).to_broadcast([P, W // RUN, PACK, RUN]),
                     op=ALU.mult)
 
@@ -161,22 +196,21 @@ def tile_eventtimestatespacedualchunk_x1_kernel(tc, cm, bm, v, dt, age, lam, h0,
                                in_=rows_view(h0_raw[:, h, :].rearrange("p (j w) -> p j w", j=PACK)))
             return h0_bf
 
-        def read_state(tg):
-            for j in range(PACK):
-                bank = psum.tile([P, H * W], F32, tag="score", bufs=2)
-                multiply(bank[:], cq[tg], block(j), hq, slice(0, H * W), True, True)
-                k = tg * PACK + j
-                for h in range(H):
-                    nc.scalar.activation(out=read[tg][:, h, j, :], in_=bank[:, block(h)], func=ACT.Copy,
-                                         scale=carry[:, h, k:k + 1])
+        def read_state(tg, j):
+            bank = psum.tile([P, H * W], F32, tag="inner", bufs=BANKS["inner"])
+            multiply(bank[:], cq[tg], block(j), hq, slice(0, H * W), True, True)
+            k = tg * PACK + j
+            for h in range(H):
+                nc.scalar.activation(out=read[tg][:, h, j, :], in_=bank[:, block(h)], func=ACT.Copy,
+                                     scale=carry[:, h, k:k + 1])
 
         def step_of(k):
-            return k // (H * GROUPS), (k // GROUPS) % H, k % GROUPS
+            return k // (H * GROUPS), (k // H) % GROUPS, k % H
 
         decay, m_bf, mq, inner, result, result_bf = {}, {}, {}, {}, {}, {}
 
         def decays(k):
-            tg, h, g = step_of(k)
+            tg, g, h = step_of(k)
             decay[k] = flow.tile([P, PACK, GROUP], F32, name="decay", tag="decay", bufs=4)
             for j in range(PACK):
                 i = g * PACK + j
@@ -184,24 +218,25 @@ def tile_eventtimestatespacedualchunk_x1_kernel(tc, cm, bm, v, dt, age, lam, h0,
                                      scale=neg_lam[:, h:h + 1], bias=lam_age[:, h, i:i + 1])
 
         def decay_scores(k):
-            tg, h, g = step_of(k)
-            m_bf[k] = flow.tile([P, GROUP * PACK], BF16, name="m_bf", tag="m_bf", bufs=3, align_bytes=64)
-            nc.vector.tensor_tensor(out=packed_view(m_bf[k][:]), in0=rows_view(masked[tg][g][:]),
-                                    in1=rows_view(decay[k][:]), op=ALU.mult)
+            m_bf[k] = flow.tile([P, PACK, P * PACK], BF16, name="m_bf", tag="m_bf", bufs=2, align_bytes=64)
+            for tile_j in range(PACK):
+                engine = nc.vector if tile_j < HELD else nc.gpsimd
+                engine.tensor_tensor(out=packed_view(m_bf[k][:, tile_j, :]), in0=rows_view(masked[k // H, tile_j][:]),
+                                     in1=rows_view(decay[k][:, :, block(tile_j)]), op=ALU.mult)
 
         def quantize_scores(k):
-            codes = flow.tile([P, GROUP], U32, name="m_codes", tag="m_codes", bufs=4, align_bytes=64)
-            scales = flow.tile([P, GROUP], U8, name="m_scales", tag="m_scales", bufs=4, align_bytes=64)
+            tg, g, h = step_of(k)
+            codes = flow.tile([P, GROUP], U32, name="m_codes", tag="m_codes", bufs=6, align_bytes=64)
+            scales = flow.tile([P, GROUP], U8, name="m_scales", tag="m_scales", bufs=6, align_bytes=64)
             mq[k] = (codes, scales)
-            quantize(codes[:], scales[:], m_bf[k][:])
-            if k % GROUPS == GROUPS - 1:
-                u = k // GROUPS
-                h = u % H
-                inner[u] = psum.tile([P, PACK, W], F32, name="inner", tag="inner", bufs=3)
+            quantize(codes[:], scales[:], m_bf[k][:].rearrange("p j x -> p (j x)"))
+            if g == GROUPS - 1:
+                u = tg * H + h
+                inner[u] = psum.tile([P, PACK, W], F32, name="inner", tag="inner", bufs=BANKS["inner"])
                 for j in range(PACK):
-                    for g in range(GROUPS):
-                        multiply(inner[u][:, j, :], mq[u * GROUPS + g], block(j), wq[h], block(g), g == 0,
-                                 g == GROUPS - 1)
+                    for gg in range(GROUPS):
+                        multiply(inner[u][:, j, :], mq[k - (GROUPS - 1 - gg) * H], block(j), wq[h], block(gg), gg == 0,
+                                 gg == GROUPS - 1)
 
         def finish(u):
             tg, h = divmod(u, H)
@@ -223,55 +258,72 @@ def tile_eventtimestatespacedualchunk_x1_kernel(tc, cm, bm, v, dt, age, lam, h0,
                     nc.sync.dma_start(out=out_2[tg, 4 * q:4 * q + 4, :].bitcast(I32),
                                       in_=scales[32 * q:32 * q + 4, :].bitcast(I32))
 
-        cm_turned = turn(cm_raw[0])
-        bm_turned = turn(bm_raw[0])
+        cm_turned = turn(cm_raw[0], "held")
+        bm_turned = turn(bm_raw[0], "held")
+        scale_values(0)
         quantize(cq[0][0][:], cq[0][1][:], cm_turned[:])
+        quantize_values(0)
         quantize(bq[0][0][:], bq[0][1][:], bm_turned[:])
         decays(0)
-        bm_turned = turn(bm_raw[1])
-        scores(0, 0, range(PACK))
+        for tile_j, tag in enumerate(("score", "inner", "inner", "score")):
+            scores(0, tile_j, tag)
+            mask_scores(0, tile_j)
+            if tile_j < HELD:
+                hold_scores(0, tile_j)
+        bm_turned = turn(bm_raw[1], "inner")
         decays(1)
         h0_bf = pack_state()
 
-        steps = GROUPS * H * GROUPS
+        steps = GROUPS * GROUPS * H
+
+        def unit_at(k, lag):
+            tg, g, h = step_of(max(k - lag, 0))
+            return tg * H + h if k >= lag and g == GROUPS - 1 else None
+
         for k in range(steps):
+            tg, g, h = step_of(k)
+            ahead = k // H + 1
+            more = ahead < GROUPS * GROUPS
+            if more and k > 0:
+                scores(ahead, h, "score")
             decay_scores(k)
-            if k + 2 < steps:
-                decays(k + 2)
+            if more and h == H - 1:
+                hold_scores(ahead, HELD - 1)
             if k == 0:
                 quantize(bq[1][0][:], bq[1][1][:], bm_turned[:])
-                cm_turned = turn(cm_raw[1])
-                scale_values(0)
-                scores(0, 1, range(PACK))
-                quantize_values(0)
+                scores(ahead, h, "score")
+                scale_values(1)
+            if k + 2 < steps:
+                decays(k + 2)
+            if unit_at(k, 2) is not None:
+                finish(unit_at(k, 2))
+            if more:
+                mask_scores(ahead, h)
+                if h < HELD - 1:
+                    hold_scores(ahead, h)
+            if k == 1:
+                cm_turned = turn(cm_raw[1], "inner")
+                quantize(hq[0][:], hq[1][:], h0_bf[:].rearrange("p h x -> p (h x)"))
+                quantize_values(1)
+            if k in (2, 4):
+                scale_values(k // 2 + 1)
+            if k in (3, 5):
+                quantize_values(k // 2 + 1)
+            if k == 3:
+                quantize(cq[1][0][:], cq[1][1][:], cm_turned[:])
+            if k in (2, 3):
+                read_state(0, 2 * k - 4)
+                read_state(0, 2 * k - 3)
+            if 9 <= k <= 12:
+                read_state(1, k - 9)
+            if unit_at(k, 3) is not None:
+                quantize_result(unit_at(k, 3))
             if k >= 1:
                 quantize_scores(k - 1)
-            if k == 1:
-                quantize(hq[0][:], hq[1][:], h0_bf[:].rearrange("p h x -> p (h x)"))
-                read_state(0)
-                scale_values(1)
-            if k == 2:
-                quantize(cq[1][0][:], cq[1][1][:], cm_turned[:])
-                quantize_values(1)
-            if k == 3:
-                scale_values(2)
-            if k == 4:
-                quantize_values(2)
-                scores(1, 0, range(0, 2))
-                scale_values(3)
-            if k == 5:
-                scores(1, 0, range(2, 4))
-            if k == 6:
-                quantize_values(3)
-                scores(1, 1, range(0, 2))
-            if k == 7:
-                scores(1, 1, range(2, 4))
-                read_state(1)
-            if k >= 3 and k % 2 == 1:
-                finish((k - 3) // 2)
-            if k >= 4 and k % 2 == 0:
-                quantize_result((k - 4) // 2)
+        last = GROUPS * H - 1
         quantize_scores(steps - 1)
-        quantize_result(GROUPS * H - 2)
-        finish(GROUPS * H - 1)
-        quantize_result(GROUPS * H - 1)
+        quantize_result(last - 2)
+        finish(last - 1)
+        finish(last)
+        quantize_result(last - 1)
+        quantize_result(last)

@@ -21,6 +21,9 @@ GROUP = P * PACK
 GROUPS = S // GROUP
 RUN = 4
 HELD = 3
+ORDER = (2, 0, 1)
+SPARE = 80
+SHARE = [16, 48, 48, 48, 48, 48, 80, 80, 80, 80, 48, 48, 8, 8, 48, 0]
 BANKS = {"held": 5, "score": 1, "inner": 2}
 
 
@@ -59,6 +62,8 @@ def tile_eventtimestatespacedualchunk_x1_kernel(tc, cm, bm, v, dt, age, lam, h0,
 
         age_col = keep.tile([P, GROUPS, PACK], BF16)
         nc.sync.dma_start(out=age_col[:], in_=age[0].rearrange("(g p j) -> p g j", p=P, j=PACK))
+        lam_all = keep.tile([P, H], BF16)
+        nc.sync.dma_start(out=lam_all[:], in_=lam.partition_broadcast(P))
 
         def load_rows(name, x, g):
             raw = keep.tile([P, PACK, N], BF16, name=name)
@@ -71,8 +76,6 @@ def tile_eventtimestatespacedualchunk_x1_kernel(tc, cm, bm, v, dt, age, lam, h0,
             return raw
 
         cm_raw = [load_rows("cm_raw0", cm, 0)]
-        lam_all = keep.tile([P, H], BF16)
-        nc.sync.dma_start(out=lam_all[:], in_=lam.partition_broadcast(P))
         bm_raw = [load_rows("bm_raw0", bm, 0)]
         dt_col = keep.tile([P, H * GROUPS, PACK], BF16)
         nc.sync.dma_start(out=dt_col[:], in_=dt[0].rearrange("h (g p j) -> p (h g) j", p=P, j=PACK))
@@ -90,12 +93,6 @@ def tile_eventtimestatespacedualchunk_x1_kernel(tc, cm, bm, v, dt, age, lam, h0,
         make_identity(nc, ident_f32[:])
 
         age_flat = age_col[:].rearrange("p g j -> p (g j)")
-        spread = psum.tile([P, S], BF16, tag="held", bufs=BANKS["held"])
-        for k in range(GROUPS * PACK):
-            nc.tensor.matmul(spread[:, block(k)], lhsT=age_flat[:, k:k + 1].to_broadcast([P, P]), rhs=ident_bf[:],
-                             start=True, stop=True)
-        age_row = keep.tile([P, S], BF16)
-        nc.vector.tensor_copy(out=age_row[:], in_=spread[:])
         lam_age = keep.tile([P, H, GROUPS * PACK], F32)
         nc.vector.tensor_tensor(
             out=lam_age[:],
@@ -108,6 +105,12 @@ def tile_eventtimestatespacedualchunk_x1_kernel(tc, cm, bm, v, dt, age, lam, h0,
         carry = keep.tile([P, H, GROUPS * PACK], F32)
         nc.scalar.activation(out=carry[:], in_=lam_age[:], func=ACT.Exp, scale=-1.0)
 
+        spread = psum.tile([P, S], BF16, tag="held", bufs=BANKS["held"])
+        for k in range(GROUPS * PACK):
+            nc.tensor.matmul(spread[:, block(k)], lhsT=age_flat[:, k:k + 1].to_broadcast([P, P]), rhs=ident_bf[:],
+                             start=True, stop=True)
+        age_row = keep.tile([P, S], BF16)
+        nc.vector.tensor_copy(out=age_row[:], in_=spread[:])
         later = keep.tile([P, GROUPS * PACK, S], BF16)
         for k in range(GROUPS * PACK):
             nc.vector.tensor_scalar(out=later[:, k, :], in0=age_row[:], scalar1=age_flat[:, k:k + 1], scalar2=None,
@@ -118,11 +121,11 @@ def tile_eventtimestatespacedualchunk_x1_kernel(tc, cm, bm, v, dt, age, lam, h0,
         wq = [operand("wq%d" % h, GROUPS * W) for h in range(H)]
         hq = operand("hq", H * W)
         oq = [operand("oq%d" % g, H * W) for g in range(GROUPS)]
-        read = [keep.tile([P, H, PACK, W], F32, name="read%d" % tg) for tg in range(GROUPS)]
+        read = [keep.tile([P, PACK, H * W], F32, name="read%d" % tg) for tg in range(GROUPS)]
 
         def turn(raw, tag):
             words = raw[:].rearrange("p j n -> p (j n)").bitcast(F32)
-            turned = flow.tile([P, GROUP * PACK], BF16, tag="turned", bufs=2, align_bytes=64)
+            turned = flow.tile([P, GROUP * PACK], BF16, tag="turned", bufs=3, align_bytes=64)
             turned_words = turned[:].bitcast(F32)
             banks = []
             for b in range(2):
@@ -137,7 +140,7 @@ def tile_eventtimestatespacedualchunk_x1_kernel(tc, cm, bm, v, dt, age, lam, h0,
                                in_=banks[b][:].rearrange("p jj u m -> p jj m u"))
             return turned
 
-        score, flipped, masked = {}, {}, {}
+        score, flipped, masked, direct = {}, {}, {}, {}
 
         def scores(group, tile_j, tag):
             tg, g = divmod(group, GROUPS)
@@ -160,19 +163,22 @@ def tile_eventtimestatespacedualchunk_x1_kernel(tc, cm, bm, v, dt, age, lam, h0,
                     in1=bank[:].rearrange("p j m -> p (j m)"), op0=ALU.is_le, op1=ALU.mult)
                 flipped[group, tile_j] = kept
             else:
-                kept = flow.tile([P, PACK, P], F32, name="direct", tag="direct", bufs=2)
+                kept = direct[group]
                 for j in range(PACK):
                     k = g * PACK + j
                     nc.vector.scalar_tensor_tensor(
-                        out=kept[:, j, :], in0=age_row[:, block(tg * PACK + tile_j)], scalar=age_flat[:, k:k + 1],
+                        out=kept[:, j, SPARE:], in0=age_row[:, block(tg * PACK + tile_j)], scalar=age_flat[:, k:k + 1],
                         in1=bank[:, j, :], op0=ALU.is_ge, op1=ALU.mult)
-                masked[group, tile_j] = kept
 
         def hold_scores(group, tile_j):
             bank = psum.tile([P, PACK, P], F32, name="held", tag="held", bufs=BANKS["held"])
             for j in range(PACK):
                 nc.tensor.transpose(bank[:, j, :], flipped[group, tile_j][:, block(j)], ident_f32[:])
             masked[group, tile_j] = bank
+
+        def copy_shared(group):
+            direct[group] = flow.tile([P, PACK, SPARE + P], F32, name="direct", tag="direct", bufs=2)
+            nc.scalar.copy(out=direct[group][:, :, :SPARE], in_=masked[group, HELD - 1][:, :, P - SPARE:])
 
         w_bf = {}
 
@@ -199,10 +205,7 @@ def tile_eventtimestatespacedualchunk_x1_kernel(tc, cm, bm, v, dt, age, lam, h0,
         def read_state(tg, j):
             bank = psum.tile([P, H * W], F32, tag="inner", bufs=BANKS["inner"])
             multiply(bank[:], cq[tg], block(j), hq, slice(0, H * W), True, True)
-            k = tg * PACK + j
-            for h in range(H):
-                nc.scalar.activation(out=read[tg][:, h, j, :], in_=bank[:, block(h)], func=ACT.Copy,
-                                     scale=carry[:, h, k:k + 1])
+            nc.scalar.copy(out=read[tg][:, j, :], in_=bank[:])
 
         def step_of(k):
             return k // (H * GROUPS), (k // H) % GROUPS, k % H
@@ -211,39 +214,54 @@ def tile_eventtimestatespacedualchunk_x1_kernel(tc, cm, bm, v, dt, age, lam, h0,
 
         def decays(k):
             tg, g, h = step_of(k)
-            decay[k] = flow.tile([P, PACK, GROUP], F32, name="decay", tag="decay", bufs=4)
+            decay[k] = flow.tile([P, PACK, GROUP], F32, name="decay", tag="decay", bufs=5)
             for j in range(PACK):
                 i = g * PACK + j
                 nc.scalar.activation(out=decay[k][:, j, :], in_=later[:, i, block(tg, GROUP)], func=ACT.Exp,
                                      scale=neg_lam[:, h:h + 1], bias=lam_age[:, h, i:i + 1])
 
         def decay_scores(k):
-            m_bf[k] = flow.tile([P, PACK, P * PACK], BF16, name="m_bf", tag="m_bf", bufs=2, align_bytes=64)
-            for tile_j in range(PACK):
-                engine = nc.vector if tile_j < HELD else nc.gpsimd
-                engine.tensor_tensor(out=packed_view(m_bf[k][:, tile_j, :]), in0=rows_view(masked[k // H, tile_j][:]),
-                                     in1=rows_view(decay[k][:, :, block(tile_j)]), op=ALU.mult)
+            group = k // H
+            low = flow.tile([P, 2 * P * PACK], BF16, name="m_low", tag="m_low", bufs=2, align_bytes=64)
+            high = flow.tile([P, 2 * P * PACK], BF16, name="m_high", tag="m_high", bufs=2, align_bytes=64)
+            m_bf[k] = (low, high)
+            split = P - SHARE[k]
+            nc.gpsimd.tensor_tensor(out=packed_view(high[:, split * PACK:]),
+                                    in0=rows_view(direct[group][:, :, SPARE - SHARE[k]:]),
+                                    in1=rows_view(decay[k][:, :, 2 * P + split:]), op=ALU.mult)
+            for tile_j in ORDER:
+                width = split if tile_j == HELD - 1 else P
+                target = high[:, :split * PACK] if tile_j == HELD - 1 else low[:, block(tile_j, P * PACK)]
+                nc.vector.tensor_tensor(out=packed_view(target), in0=rows_view(masked[group, tile_j][:, :, :width]),
+                                        in1=rows_view(decay[k][:, :, tile_j * P:tile_j * P + width]), op=ALU.mult)
 
         def quantize_scores(k):
             tg, g, h = step_of(k)
             codes = flow.tile([P, GROUP], U32, name="m_codes", tag="m_codes", bufs=6, align_bytes=64)
             scales = flow.tile([P, GROUP], U8, name="m_scales", tag="m_scales", bufs=6, align_bytes=64)
             mq[k] = (codes, scales)
-            quantize(codes[:], scales[:], m_bf[k][:].rearrange("p j x -> p (j x)"))
+            for half in (1, 0):
+                quantize(codes[:, block(half, 2 * P)], scales[:, block(half, 2 * P)], m_bf[k][half][:])
             if g == GROUPS - 1:
                 u = tg * H + h
-                inner[u] = psum.tile([P, PACK, W], F32, name="inner", tag="inner", bufs=BANKS["inner"])
+                tag = "score" if u == GROUPS * H - 1 else "inner"
+                inner[u] = psum.tile([P, PACK, W], F32, name="inner", tag=tag, bufs=BANKS[tag])
                 for j in range(PACK):
                     for gg in range(GROUPS):
                         multiply(inner[u][:, j, :], mq[k - (GROUPS - 1 - gg) * H], block(j), wq[h], block(gg), gg == 0,
                                  gg == GROUPS - 1)
 
-        def finish(u):
+        def finish(u, on_vector=False):
             tg, h = divmod(u, H)
-            result[u] = flow.tile([P, PACK, W], F32, name="result", tag="result", bufs=3)
-            nc.vector.tensor_tensor(out=result[u][:], in0=inner[u][:], in1=read[tg][:, h, :, :], op=ALU.add)
-            result_bf[u] = flow.tile([P, W * PACK], BF16, name="result_bf", tag="result_bf", bufs=2, align_bytes=64)
-            nc.scalar.copy(out=packed_view(result_bf[u][:]), in_=rows_view(result[u][:]))
+            result[u] = flow.tile([P, PACK, W], F32, name="result", tag="result", bufs=4)
+            result_bf[u] = flow.tile([P, W * PACK], BF16, name="result_bf", tag="result_bf", bufs=4, align_bytes=64)
+            for j in range(PACK):
+                k = tg * PACK + j
+                nc.vector.scalar_tensor_tensor(out=result[u][:, j, :], in0=read[tg][:, j, block(h)],
+                                               scalar=carry[:, h, k:k + 1], in1=inner[u][:, j, :],
+                                               op0=ALU.mult, op1=ALU.add)
+            if not on_vector:
+                nc.scalar.copy(out=packed_view(result_bf[u][:]), in_=rows_view(result[u][:]))
             nc.sync.dma_start(out=out_0[0, h, block(tg, GROUP), :].rearrange("(p j) w -> p j w", j=PACK),
                               in_=result[u][:])
 
@@ -255,24 +273,30 @@ def tile_eventtimestatespacedualchunk_x1_kernel(tc, cm, bm, v, dt, age, lam, h0,
                               in_=codes[:, block(h)].bitcast(I32))
             if h == H - 1:
                 for q in range(4):
-                    nc.sync.dma_start(out=out_2[tg, 4 * q:4 * q + 4, :].bitcast(I32),
-                                      in_=scales[32 * q:32 * q + 4, :].bitcast(I32))
+                    queue = nc.scalar if q % 2 == 0 and tg == GROUPS - 1 else nc.sync
+                    queue.dma_start(out=out_2[tg, 4 * q:4 * q + 4, :].bitcast(I32),
+                                    in_=scales[32 * q:32 * q + 4, :].bitcast(I32))
 
         cm_turned = turn(cm_raw[0], "held")
         bm_turned = turn(bm_raw[0], "held")
-        scale_values(0)
         quantize(cq[0][0][:], cq[0][1][:], cm_turned[:])
-        quantize_values(0)
         quantize(bq[0][0][:], bq[0][1][:], bm_turned[:])
+        scale_values(0)
+        bm_later = turn(bm_raw[1], "held")
         decays(0)
-        for tile_j, tag in enumerate(("score", "inner", "inner", "score")):
+        tiles = ORDER + (HELD,)
+        for tile_j, tag in zip(tiles, ("score", "inner", "inner", "held")):
             scores(0, tile_j, tag)
+        for tile_j in ORDER:
             mask_scores(0, tile_j)
-            if tile_j < HELD:
-                hold_scores(0, tile_j)
-        bm_turned = turn(bm_raw[1], "inner")
+            hold_scores(0, tile_j)
+            if tile_j == HELD - 1:
+                copy_shared(0)
         decays(1)
-        h0_bf = pack_state()
+        quantize_values(0)
+        quantize(bq[1][0][:], bq[1][1][:], bm_later[:])
+        mask_scores(0, HELD)
+        decays(2)
 
         steps = GROUPS * GROUPS * H
 
@@ -284,46 +308,52 @@ def tile_eventtimestatespacedualchunk_x1_kernel(tc, cm, bm, v, dt, age, lam, h0,
             tg, g, h = step_of(k)
             ahead = k // H + 1
             more = ahead < GROUPS * GROUPS
-            if more and k > 0:
-                scores(ahead, h, "score")
+            if more:
+                scores(ahead, tiles[h], "score")
             decay_scores(k)
+            if k == steps - 1:
+                break
             if more and h == H - 1:
-                hold_scores(ahead, HELD - 1)
+                hold_scores(ahead, ORDER[-1])
             if k == 0:
-                quantize(bq[1][0][:], bq[1][1][:], bm_turned[:])
-                scores(ahead, h, "score")
-                scale_values(1)
-            if k + 2 < steps:
-                decays(k + 2)
+                h0_bf = pack_state()
+            if k + 3 < steps:
+                decays(k + 3)
             if unit_at(k, 2) is not None:
                 finish(unit_at(k, 2))
             if more:
-                mask_scores(ahead, h)
+                if h == 1:
+                    copy_shared(ahead)
+                mask_scores(ahead, tiles[h])
                 if h < HELD - 1:
-                    hold_scores(ahead, h)
+                    hold_scores(ahead, tiles[h])
             if k == 1:
                 cm_turned = turn(cm_raw[1], "inner")
+            if 1 <= k < H:
+                scale_values(k)
+            if k == 2:
                 quantize(hq[0][:], hq[1][:], h0_bf[:].rearrange("p h x -> p (h x)"))
-                quantize_values(1)
-            if k in (2, 4):
-                scale_values(k // 2 + 1)
-            if k in (3, 5):
-                quantize_values(k // 2 + 1)
+            if 2 <= k <= H:
+                quantize_values(k - 1)
             if k == 3:
                 quantize(cq[1][0][:], cq[1][1][:], cm_turned[:])
-            if k in (2, 3):
-                read_state(0, 2 * k - 4)
-                read_state(0, 2 * k - 3)
+            if k in (3, 4):
+                read_state(0, 2 * k - 6)
+                read_state(0, 2 * k - 5)
             if 9 <= k <= 12:
                 read_state(1, k - 9)
-            if unit_at(k, 3) is not None:
-                quantize_result(unit_at(k, 3))
+            if unit_at(k, 4) is not None:
+                quantize_result(unit_at(k, 4))
             if k >= 1:
                 quantize_scores(k - 1)
         last = GROUPS * H - 1
+        quantize_scores(steps - 2)
         quantize_scores(steps - 1)
-        quantize_result(last - 2)
+        finish(last - 2)
         finish(last - 1)
-        finish(last)
+        quantize_result(last - 3)
+        finish(last, on_vector=True)
+        quantize_result(last - 2)
+        nc.vector.tensor_copy(out=packed_view(result_bf[last][:]), in_=rows_view(result[last][:]))
         quantize_result(last - 1)
         quantize_result(last)

@@ -22,8 +22,9 @@ GROUPS = S // GROUP
 RUN = 4
 HELD = 3
 ORDER = (2, 0, 1)
-SPARE = 80
-SHARE = [16, 48, 48, 48, 48, 48, 80, 80, 80, 80, 48, 48, 8, 8, 48, 0]
+CFG = {"bm1first": 1, "w1g": 1, "lead": 3, "read": [3, 3, 4, 4, 10, 10, 11, 11], "cm1": 1, "round": [6, 7, 8, 9, 14], "early": 0, "pack": 0, "shared": 1, "w": [0, 1, 2, 3], "wq": [0, 2, 3, 4], "hq": 2, "cq1": 3, "q": [8, 9, 10, 11], "share": [0, 24, 48, 56, 56, 56, 80, 80, 80, 80, 56, 56, 8, 8, 56, 8]}
+SHARE = CFG["share"]
+SPARE = max(SHARE)
 BANKS = {"held": 5, "score": 1, "inner": 2}
 
 
@@ -54,11 +55,11 @@ def tile_eventtimestatespacedualchunk_x1_kernel(tc, cm, bm, v, dt, age, lam, h0,
         def block(i, width=P):
             return slice(i * width, (i + 1) * width)
 
-        def rows_view(ap):
-            return ap.rearrange("p j (c i) -> p c j i", i=RUN)
+        def rows_view(ap, run=RUN):
+            return ap.rearrange("p j (c i) -> p c j i", i=run)
 
-        def packed_view(ap):
-            return ap.rearrange("p (c i j) -> p c j i", i=RUN, j=PACK)
+        def packed_view(ap, run=RUN):
+            return ap.rearrange("p (c i j) -> p c j i", i=run, j=PACK)
 
         age_col = keep.tile([P, GROUPS, PACK], BF16)
         nc.sync.dma_start(out=age_col[:], in_=age[0].rearrange("(g p j) -> p g j", p=P, j=PACK))
@@ -123,10 +124,8 @@ def tile_eventtimestatespacedualchunk_x1_kernel(tc, cm, bm, v, dt, age, lam, h0,
         oq = [operand("oq%d" % g, H * W) for g in range(GROUPS)]
         read = [keep.tile([P, PACK, H * W], F32, name="read%d" % tg) for tg in range(GROUPS)]
 
-        def turn(raw, tag):
+        def turn_a(raw, tag):
             words = raw[:].rearrange("p j n -> p (j n)").bitcast(F32)
-            turned = flow.tile([P, GROUP * PACK], BF16, tag="turned", bufs=3, align_bytes=64)
-            turned_words = turned[:].bitcast(F32)
             banks = []
             for b in range(2):
                 bank = psum.tile([P, 2, 2, P], F32, tag=tag, bufs=BANKS[tag])
@@ -135,10 +134,18 @@ def tile_eventtimestatespacedualchunk_x1_kernel(tc, cm, bm, v, dt, age, lam, h0,
                     for u in range(2):
                         nc.tensor.transpose(bank[:, jj, u, :], words[:, 256 * j + u:256 * (j + 1):2], ident_f32[:])
                 banks.append(bank)
+            return banks
+
+        def turn_b(banks):
+            turned = flow.tile([P, GROUP * PACK], BF16, tag="turned", bufs=3, align_bytes=64)
+            turned_words = turned[:].bitcast(F32)
             for b in range(2):
                 nc.scalar.copy(out=turned_words[:, block(b, GROUP)].rearrange("p (jj m u) -> p jj m u", jj=2, u=2),
                                in_=banks[b][:].rearrange("p jj u m -> p jj m u"))
             return turned
+
+        def turn(raw, tag):
+            return turn_b(turn_a(raw, tag))
 
         score, flipped, masked, direct = {}, {}, {}, {}
 
@@ -180,13 +187,14 @@ def tile_eventtimestatespacedualchunk_x1_kernel(tc, cm, bm, v, dt, age, lam, h0,
             direct[group] = flow.tile([P, PACK, SPARE + P], F32, name="direct", tag="direct", bufs=2)
             nc.scalar.copy(out=direct[group][:, :, :SPARE], in_=masked[group, HELD - 1][:, :, P - SPARE:])
 
-        w_bf = {}
+        w_bf, state_bank = {}, {}
 
-        def scale_values(h):
-            w_bf[h] = flow.tile([P, GROUPS, W * PACK], BF16, name="w_bf", tag="w_bf", bufs=2, align_bytes=64)
+        def scale_values(h, engine):
+            tag = "w_first" if h < 2 else "w%d" % h
+            w_bf[h] = flow.tile([P, GROUPS, W * PACK], BF16, name="w_bf", tag=tag, bufs=1, align_bytes=64)
             for g in range(GROUPS):
                 hg = h * GROUPS + g
-                nc.vector.tensor_tensor(
+                engine.tensor_tensor(
                     out=packed_view(w_bf[h][:, g, :]),
                     in0=rows_view(v_raw[h][:, g, :].rearrange("p (j w) -> p j w", j=PACK)),
                     in1=dt_col[:, hg, :].unsqueeze(1).unsqueeze(3).to_broadcast([P, W // RUN, PACK, RUN]),
@@ -205,7 +213,10 @@ def tile_eventtimestatespacedualchunk_x1_kernel(tc, cm, bm, v, dt, age, lam, h0,
         def read_state(tg, j):
             bank = psum.tile([P, H * W], F32, tag="inner", bufs=BANKS["inner"])
             multiply(bank[:], cq[tg], block(j), hq, slice(0, H * W), True, True)
-            nc.scalar.copy(out=read[tg][:, j, :], in_=bank[:])
+            state_bank[tg, j] = bank
+
+        def copy_state(tg, j):
+            nc.scalar.copy(out=read[tg][:, j, :], in_=state_bank[tg, j][:])
 
         def step_of(k):
             return k // (H * GROUPS), (k // H) % GROUPS, k % H
@@ -214,7 +225,7 @@ def tile_eventtimestatespacedualchunk_x1_kernel(tc, cm, bm, v, dt, age, lam, h0,
 
         def decays(k):
             tg, g, h = step_of(k)
-            decay[k] = flow.tile([P, PACK, GROUP], F32, name="decay", tag="decay", bufs=5)
+            decay[k] = flow.tile([P, PACK, GROUP], F32, name="decay", tag="decay", bufs=CFG["lead"] + 2)
             for j in range(PACK):
                 i = g * PACK + j
                 nc.scalar.activation(out=decay[k][:, j, :], in_=later[:, i, block(tg, GROUP)], func=ACT.Exp,
@@ -232,8 +243,8 @@ def tile_eventtimestatespacedualchunk_x1_kernel(tc, cm, bm, v, dt, age, lam, h0,
             for tile_j in ORDER:
                 width = split if tile_j == HELD - 1 else P
                 target = high[:, :split * PACK] if tile_j == HELD - 1 else low[:, block(tile_j, P * PACK)]
-                nc.vector.tensor_tensor(out=packed_view(target), in0=rows_view(masked[group, tile_j][:, :, :width]),
-                                        in1=rows_view(decay[k][:, :, tile_j * P:tile_j * P + width]), op=ALU.mult)
+                nc.vector.tensor_tensor(out=packed_view(target, 2), in0=rows_view(masked[group, tile_j][:, :, :width], 2),
+                                        in1=rows_view(decay[k][:, :, tile_j * P:tile_j * P + width], 2), op=ALU.mult)
 
         def quantize_scores(k):
             tg, g, h = step_of(k)
@@ -251,19 +262,20 @@ def tile_eventtimestatespacedualchunk_x1_kernel(tc, cm, bm, v, dt, age, lam, h0,
                         multiply(inner[u][:, j, :], mq[k - (GROUPS - 1 - gg) * H], block(j), wq[h], block(gg), gg == 0,
                                  gg == GROUPS - 1)
 
-        def finish(u, on_vector=False):
+        def finish(u):
             tg, h = divmod(u, H)
-            result[u] = flow.tile([P, PACK, W], F32, name="result", tag="result", bufs=4)
-            result_bf[u] = flow.tile([P, W * PACK], BF16, name="result_bf", tag="result_bf", bufs=4, align_bytes=64)
+            result[u] = flow.tile([P, PACK, W], F32, name="result", tag="result", bufs=8)
             for j in range(PACK):
                 k = tg * PACK + j
                 nc.vector.scalar_tensor_tensor(out=result[u][:, j, :], in0=read[tg][:, j, block(h)],
                                                scalar=carry[:, h, k:k + 1], in1=inner[u][:, j, :],
                                                op0=ALU.mult, op1=ALU.add)
-            if not on_vector:
-                nc.scalar.copy(out=packed_view(result_bf[u][:]), in_=rows_view(result[u][:]))
             nc.sync.dma_start(out=out_0[0, h, block(tg, GROUP), :].rearrange("(p j) w -> p j w", j=PACK),
                               in_=result[u][:])
+
+        def round_result(u, copy):
+            result_bf[u] = flow.tile([P, W * PACK], BF16, name="result_bf", tag="result_bf", bufs=6, align_bytes=64)
+            copy(out=packed_view(result_bf[u][:]), in_=rows_view(result[u][:]))
 
         def quantize_result(u):
             tg, h = divmod(u, H)
@@ -281,22 +293,29 @@ def tile_eventtimestatespacedualchunk_x1_kernel(tc, cm, bm, v, dt, age, lam, h0,
         bm_turned = turn(bm_raw[0], "held")
         quantize(cq[0][0][:], cq[0][1][:], cm_turned[:])
         quantize(bq[0][0][:], bq[0][1][:], bm_turned[:])
-        scale_values(0)
+        scale_values(0, nc.vector)
+        if not CFG["bm1first"]:
+            decays(0)
         bm_later = turn(bm_raw[1], "held")
-        decays(0)
+        if CFG["bm1first"]:
+            decays(0)
         tiles = ORDER + (HELD,)
         for tile_j, tag in zip(tiles, ("score", "inner", "inner", "held")):
             scores(0, tile_j, tag)
-        for tile_j in ORDER:
+        for tile_j in ORDER[:2]:
             mask_scores(0, tile_j)
             hold_scores(0, tile_j)
-            if tile_j == HELD - 1:
-                copy_shared(0)
+        copy_shared(0)
         decays(1)
-        quantize_values(0)
         quantize(bq[1][0][:], bq[1][1][:], bm_later[:])
+        quantize_values(0)
+        if CFG["w1g"]:
+            scale_values(1, nc.gpsimd)
+        mask_scores(0, ORDER[2])
+        hold_scores(0, ORDER[2])
         mask_scores(0, HELD)
-        decays(2)
+        for k in range(2, CFG["lead"]):
+            decays(k)
 
         steps = GROUPS * GROUPS * H
 
@@ -310,50 +329,64 @@ def tile_eventtimestatespacedualchunk_x1_kernel(tc, cm, bm, v, dt, age, lam, h0,
             more = ahead < GROUPS * GROUPS
             if more:
                 scores(ahead, tiles[h], "score")
+            for i in range(8):
+                if CFG["read"][i] == k:
+                    read_state(i // 4, i % 4)
+            if k == CFG["cm1"]:
+                cm_banks = turn_a(cm_raw[1], "inner")
             decay_scores(k)
             if k == steps - 1:
                 break
             if more and h == H - 1:
                 hold_scores(ahead, ORDER[-1])
-            if k == 0:
+            if k == CFG["cm1"]:
+                cm_turned = turn_b(cm_banks)
+            for i in range(8):
+                if CFG["read"][i] == k:
+                    copy_state(i // 4, i % 4)
+            for u in range(5):
+                if CFG["round"][u] == k and CFG["early"] and u < 4:
+                    round_result(u, nc.scalar.copy)
+            if k + CFG["lead"] < steps:
+                decays(k + CFG["lead"])
+            if k == CFG["pack"]:
                 h0_bf = pack_state()
-            if k + 3 < steps:
-                decays(k + 3)
             if unit_at(k, 2) is not None:
                 finish(unit_at(k, 2))
+            for u in range(5):
+                if CFG["round"][u] == k and (u == 4 or not CFG["early"]):
+                    round_result(u, nc.scalar.copy)
             if more:
-                if h == 1:
+                if h == CFG["shared"]:
                     copy_shared(ahead)
                 mask_scores(ahead, tiles[h])
                 if h < HELD - 1:
                     hold_scores(ahead, tiles[h])
-            if k == 1:
-                cm_turned = turn(cm_raw[1], "inner")
-            if 1 <= k < H:
-                scale_values(k)
-            if k == 2:
+            for hh in range(1, H):
+                if CFG["wq"][hh] == k:
+                    quantize_values(hh)
+            for hh in range(1, H):
+                if CFG["w"][hh] == k and not (hh == 1 and CFG["w1g"]):
+                    scale_values(hh, nc.vector)
+            if k == CFG["hq"]:
                 quantize(hq[0][:], hq[1][:], h0_bf[:].rearrange("p h x -> p (h x)"))
-            if 2 <= k <= H:
-                quantize_values(k - 1)
-            if k == 3:
+            if k == CFG["cq1"]:
                 quantize(cq[1][0][:], cq[1][1][:], cm_turned[:])
-            if k in (3, 4):
-                read_state(0, 2 * k - 6)
-                read_state(0, 2 * k - 5)
-            if 9 <= k <= 12:
-                read_state(1, k - 9)
-            if unit_at(k, 4) is not None:
-                quantize_result(unit_at(k, 4))
+            for u in range(4):
+                if CFG["q"][u] == k:
+                    quantize_result(u)
             if k >= 1:
                 quantize_scores(k - 1)
         last = GROUPS * H - 1
         quantize_scores(steps - 2)
         quantize_scores(steps - 1)
         finish(last - 2)
+        round_result(last - 2, nc.scalar.copy)
         finish(last - 1)
+        round_result(last - 1, nc.scalar.copy)
         quantize_result(last - 3)
-        finish(last, on_vector=True)
+        finish(last)
         quantize_result(last - 2)
-        nc.vector.tensor_copy(out=packed_view(result_bf[last][:]), in_=rows_view(result[last][:]))
+        round_result(last, nc.vector.tensor_copy)
         quantize_result(last - 1)
         quantize_result(last)

@@ -19,13 +19,56 @@ P = 128
 PACK = 4
 GROUP = P * PACK
 GROUPS = S // GROUP
-RUN = 4
-HELD = 3
-ORDER = (2, 0, 1)
-CFG = {"bm1first": 1, "w1g": 1, "lead": 3, "read": [3, 3, 4, 4, 10, 10, 11, 11], "cm1": 1, "round": [6, 7, 8, 9, 14], "early": 0, "pack": 0, "shared": 1, "w": [0, 1, 2, 3], "wq": [0, 2, 3, 4], "hq": 2, "cq1": 3, "q": [8, 9, 10, 11], "share": [0, 24, 48, 56, 56, 56, 80, 80, 80, 80, 56, 56, 8, 8, 56, 8]}
-SHARE = CFG["share"]
-SPARE = max(SHARE)
+TILES = GROUPS * PACK
+STEPS = GROUPS * GROUPS * H
+UNITS = GROUPS * H
+
+SHARED_TILE, SBUF_TILE = 2, 3
+HELD_ORDER = (SHARED_TILE, 0, 1)
+TILE_ORDER = HELD_ORDER + (SBUF_TILE,)
+
+SHARE_BY_READERS = (8, 56, 96)
+SPARE = max(SHARE_BY_READERS)
+
 BANKS = {"held": 5, "score": 1, "inner": 2}
+
+DECAY_LEAD = 3
+FINISH_LAG = 2
+PLANES_LAG = 4
+
+PACK_STATE_STEP, TURN_CM_STEP, QUANTIZE_STATE_STEP, QUANTIZE_CM_STEP = 0, 2, 2, 3
+READ_STATE_STEPS = (3, 3, 4, 4, 10, 10, 11, 12)
+
+
+def step_of(k):
+    return k // (H * GROUPS), (k // H) % GROUPS, k % H
+
+
+def unit_closed_by(k):
+    if k < 0:
+        return None
+    target_group, source_group, head = step_of(k)
+    return target_group * H + head if source_group == GROUPS - 1 else None
+
+
+def share_of(k):
+    if k < 2:
+        return 0
+    has_mask = k < STEPS - H
+    has_sum = unit_closed_by(k - FINISH_LAG) is not None and k < STEPS - 1
+    return SHARE_BY_READERS[int(has_mask) + int(has_sum)]
+
+
+def block(i, width=P):
+    return slice(i * width, (i + 1) * width)
+
+
+def rows_view(ap, run=4):
+    return ap.rearrange("p j (c i) -> p c j i", i=run)
+
+
+def packed_view(ap, run=4):
+    return ap.rearrange("p (c i j) -> p c j i", i=run, j=PACK)
 
 
 def tile_eventtimestatespacedualchunk_x1_kernel(tc, cm, bm, v, dt, age, lam, h0, out_0, out_1, out_2):
@@ -36,35 +79,25 @@ def tile_eventtimestatespacedualchunk_x1_kernel(tc, cm, bm, v, dt, age, lam, h0,
         psum = ctx.enter_context(tc.psum_pool(name="psum", bufs=2))
         ctx.enter_context(tc.manual_schedule())
 
+        def bank_tile(shape, dtype, tag):
+            return psum.tile(shape, dtype, name=tag, tag=tag, bufs=BANKS[tag])
+
         def operand(name, width):
             codes = keep.tile([P, width], U32, name=name + "_codes", align_bytes=64)
             scales = keep.tile([P, width], U8, name=name + "_scales", align_bytes=64)
             return codes, scales
 
-        def quantize(codes, scales, values):
-            nc.vector.quantize_mx(out=codes.bitcast(FP8X4), scales=scales, in_=values)
+        def quantize(target, cols, values):
+            codes, scales = target
+            nc.vector.quantize_mx(out=codes[:, cols].bitcast(FP8X4), scales=scales[:, cols], in_=values)
 
-        def multiply(acc, lhs, lhs_cols, rhs, rhs_cols, start, stop):
+        def multiply(acc, lhs, lhs_cols, rhs, rhs_cols, start=True, stop=True):
             nc.tensor.matmul_mx(
                 out=acc,
                 lhsT=lhs[0][:, lhs_cols].bitcast(FP8X4), lhsT_scale=lhs[1][:, lhs_cols],
                 rhs=rhs[0][:, rhs_cols].bitcast(FP8X4), rhs_scale=rhs[1][:, rhs_cols],
                 start=start, stop=stop,
             )
-
-        def block(i, width=P):
-            return slice(i * width, (i + 1) * width)
-
-        def rows_view(ap, run=RUN):
-            return ap.rearrange("p j (c i) -> p c j i", i=run)
-
-        def packed_view(ap, run=RUN):
-            return ap.rearrange("p (c i j) -> p c j i", i=run, j=PACK)
-
-        age_col = keep.tile([P, GROUPS, PACK], BF16)
-        nc.sync.dma_start(out=age_col[:], in_=age[0].rearrange("(g p j) -> p g j", p=P, j=PACK))
-        lam_all = keep.tile([P, H], BF16)
-        nc.sync.dma_start(out=lam_all[:], in_=lam.partition_broadcast(P))
 
         def load_rows(name, x, g):
             raw = keep.tile([P, PACK, N], BF16, name=name)
@@ -76,16 +109,23 @@ def tile_eventtimestatespacedualchunk_x1_kernel(tc, cm, bm, v, dt, age, lam, h0,
             nc.sync.dma_start(out=raw[:], in_=v[0, h].rearrange("(g p j) w -> p g (j w)", p=P, j=PACK))
             return raw
 
-        cm_raw = [load_rows("cm_raw0", cm, 0)]
+        age_col = keep.tile([P, GROUPS, PACK], BF16)
+        nc.sync.dma_start(out=age_col[:], in_=age[0].rearrange("(g p j) -> p g j", p=P, j=PACK))
+        lam_all = keep.tile([P, H], BF16)
+        nc.sync.dma_start(out=lam_all[:], in_=lam.partition_broadcast(P))
         bm_raw = [load_rows("bm_raw0", bm, 0)]
-        dt_col = keep.tile([P, H * GROUPS, PACK], BF16)
-        nc.sync.dma_start(out=dt_col[:], in_=dt[0].rearrange("h (g p j) -> p (h g) j", p=P, j=PACK))
-        v_raw = [load_values(0)]
+        cm_raw = [load_rows("cm_raw0", cm, 0)]
         bm_raw.append(load_rows("bm_raw1", bm, 1))
+        dt_first = keep.tile([P, GROUPS, PACK], BF16)
+        nc.sync.dma_start(out=dt_first[:], in_=dt[0, 0].rearrange("(g p j) -> p g j", p=P, j=PACK))
+        v_raw = [load_values(0)]
+        dt_rest = keep.tile([P, (H - 1) * GROUPS, PACK], BF16)
+        nc.sync.dma_start(out=dt_rest[:], in_=dt[0, 1:].rearrange("h (g p j) -> p (h g) j", p=P, j=PACK))
+        v_raw.append(load_values(1))
         h0_raw = keep.tile([P, H, PACK * W], BF16)
         nc.sync.dma_start(out=h0_raw[:], in_=h0[0].rearrange("h (p j) w -> p h (j w)", j=PACK))
         cm_raw.append(load_rows("cm_raw1", cm, 1))
-        for h in range(1, H):
+        for h in range(2, H):
             v_raw.append(load_values(h))
 
         ident_bf = keep.tile([P, P], BF16)
@@ -93,297 +133,275 @@ def tile_eventtimestatespacedualchunk_x1_kernel(tc, cm, bm, v, dt, age, lam, h0,
         ident_f32 = keep.tile([P, P], F32)
         make_identity(nc, ident_f32[:])
 
-        age_flat = age_col[:].rearrange("p g j -> p (g j)")
-        lam_age = keep.tile([P, H, GROUPS * PACK], F32)
+        age_tiles = age_col[:].rearrange("p g j -> p (g j)")
+        lam_age = keep.tile([P, H, TILES], F32)
         nc.vector.tensor_tensor(
             out=lam_age[:],
-            in0=age_flat.unsqueeze(1).to_broadcast([P, H, GROUPS * PACK]),
-            in1=lam_all[:].unsqueeze(2).to_broadcast([P, H, GROUPS * PACK]),
+            in0=age_tiles.unsqueeze(1).to_broadcast([P, H, TILES]),
+            in1=lam_all[:].unsqueeze(2).to_broadcast([P, H, TILES]),
             op=ALU.mult,
         )
         neg_lam = keep.tile([P, H], F32)
         nc.vector.tensor_scalar(out=neg_lam[:], in0=lam_all[:], scalar1=-1.0, scalar2=None, op0=ALU.mult)
-        carry = keep.tile([P, H, GROUPS * PACK], F32)
+        carry = keep.tile([P, H, TILES], F32)
         nc.scalar.activation(out=carry[:], in_=lam_age[:], func=ACT.Exp, scale=-1.0)
 
-        spread = psum.tile([P, S], BF16, tag="held", bufs=BANKS["held"])
-        for k in range(GROUPS * PACK):
-            nc.tensor.matmul(spread[:, block(k)], lhsT=age_flat[:, k:k + 1].to_broadcast([P, P]), rhs=ident_bf[:],
+        spread = bank_tile([P, S], BF16, "held")
+        for i in range(TILES):
+            nc.tensor.matmul(spread[:, block(i)], lhsT=age_tiles[:, i:i + 1].to_broadcast([P, P]), rhs=ident_bf[:],
                              start=True, stop=True)
         age_row = keep.tile([P, S], BF16)
         nc.vector.tensor_copy(out=age_row[:], in_=spread[:])
-        later = keep.tile([P, GROUPS * PACK, S], BF16)
-        for k in range(GROUPS * PACK):
-            nc.vector.tensor_scalar(out=later[:, k, :], in0=age_row[:], scalar1=age_flat[:, k:k + 1], scalar2=None,
-                                    op0=ALU.max)
 
         cq = [operand("cq%d" % g, GROUP) for g in range(GROUPS)]
         bq = [operand("bq%d" % g, GROUP) for g in range(GROUPS)]
         wq = [operand("wq%d" % h, GROUPS * W) for h in range(H)]
         hq = operand("hq", H * W)
-        oq = [operand("oq%d" % g, H * W) for g in range(GROUPS)]
-        read = [keep.tile([P, PACK, H * W], F32, name="read%d" % tg) for tg in range(GROUPS)]
+        planes = [operand("planes%d" % g, H * W) for g in range(GROUPS)]
+        later = keep.tile([P, TILES, S], BF16)
+        state_read = [keep.tile([P, PACK, H * W], F32, name="state_read%d" % g) for g in range(GROUPS)]
+        score, flipped, held, in_sbuf, state_bank = {}, {}, {}, {}, {}
+        w_bf, decay, m_bf, mq, inner, result, result_bf = {}, {}, {}, {}, {}, {}, {}
 
-        def turn_a(raw, tag):
+        def transpose_rows(raw, tag, bank_order=(0, 1)):
             words = raw[:].rearrange("p j n -> p (j n)").bitcast(F32)
-            banks = []
-            for b in range(2):
-                bank = psum.tile([P, 2, 2, P], F32, tag=tag, bufs=BANKS[tag])
+            row_words = N // 2
+            banks = {}
+            for b in bank_order:
+                bank = bank_tile([P, 2, 2, P], F32, tag)
                 for jj in range(2):
                     j = 2 * b + jj
                     for u in range(2):
-                        nc.tensor.transpose(bank[:, jj, u, :], words[:, 256 * j + u:256 * (j + 1):2], ident_f32[:])
-                banks.append(bank)
+                        nc.tensor.transpose(bank[:, jj, u, :], words[:, row_words * j + u:row_words * (j + 1):2],
+                                            ident_f32[:])
+                banks[b] = bank
             return banks
 
-        def turn_b(banks):
+        def pack_rows(banks):
             turned = flow.tile([P, GROUP * PACK], BF16, tag="turned", bufs=3, align_bytes=64)
             turned_words = turned[:].bitcast(F32)
-            for b in range(2):
+            for b in banks:
                 nc.scalar.copy(out=turned_words[:, block(b, GROUP)].rearrange("p (jj m u) -> p jj m u", jj=2, u=2),
                                in_=banks[b][:].rearrange("p jj u m -> p jj m u"))
             return turned
 
-        def turn(raw, tag):
-            return turn_b(turn_a(raw, tag))
-
-        score, flipped, masked, direct = {}, {}, {}, {}
-
-        def scores(group, tile_j, tag):
-            tg, g = divmod(group, GROUPS)
-            bank = psum.tile([P, PACK, P], F32, name="score", tag=tag, bufs=BANKS[tag])
-            score[group, tile_j] = bank
-            if tile_j < HELD:
-                multiply(bank[:].rearrange("p j m -> p (j m)"), cq[tg], block(tile_j), bq[g], slice(0, GROUP), True, True)
-            else:
+        def scores(pair, t, tag):
+            target_group, source_group = divmod(pair, GROUPS)
+            bank = bank_tile([P, PACK, P], F32, tag)
+            score[pair, t] = bank
+            if t == SBUF_TILE:
                 for j in range(PACK):
-                    multiply(bank[:, j, :], bq[g], block(j), cq[tg], block(tile_j), True, True)
-
-        def mask_scores(group, tile_j):
-            tg, g = divmod(group, GROUPS)
-            bank = score[group, tile_j]
-            if tile_j < HELD:
-                k = tg * PACK + tile_j
-                kept = flow.tile([P, GROUP], F32, name="flipped", tag="flipped", bufs=3)
-                nc.vector.scalar_tensor_tensor(
-                    out=kept[:], in0=age_row[:, block(g, GROUP)], scalar=age_flat[:, k:k + 1],
-                    in1=bank[:].rearrange("p j m -> p (j m)"), op0=ALU.is_le, op1=ALU.mult)
-                flipped[group, tile_j] = kept
+                    multiply(bank[:, j, :], bq[source_group], block(j), cq[target_group], block(t))
             else:
-                kept = direct[group]
+                multiply(bank[:].rearrange("p j m -> p (j m)"), cq[target_group], block(t), bq[source_group],
+                         block(0, GROUP))
+
+        def mask_scores(pair, t):
+            target_group, source_group = divmod(pair, GROUPS)
+            bank = score[pair, t]
+            target_tile = target_group * PACK + t
+            if t == SBUF_TILE:
                 for j in range(PACK):
-                    k = g * PACK + j
+                    i = source_group * PACK + j
                     nc.vector.scalar_tensor_tensor(
-                        out=kept[:, j, SPARE:], in0=age_row[:, block(tg * PACK + tile_j)], scalar=age_flat[:, k:k + 1],
-                        in1=bank[:, j, :], op0=ALU.is_ge, op1=ALU.mult)
+                        out=in_sbuf[pair][:, j, SPARE:], in0=age_row[:, block(target_tile)],
+                        scalar=age_tiles[:, i:i + 1], in1=bank[:, j, :], op0=ALU.is_ge, op1=ALU.mult)
+            else:
+                flipped[pair, t] = flow.tile([P, GROUP], F32, name="flipped", tag="flipped", bufs=3)
+                nc.vector.scalar_tensor_tensor(
+                    out=flipped[pair, t][:], in0=age_row[:, block(source_group, GROUP)],
+                    scalar=age_tiles[:, target_tile:target_tile + 1], in1=bank[:].rearrange("p j m -> p (j m)"),
+                    op0=ALU.is_le, op1=ALU.mult)
 
-        def hold_scores(group, tile_j):
-            bank = psum.tile([P, PACK, P], F32, name="held", tag="held", bufs=BANKS["held"])
+        def hold_scores(pair, t):
+            bank = bank_tile([P, PACK, P], F32, "held")
             for j in range(PACK):
-                nc.tensor.transpose(bank[:, j, :], flipped[group, tile_j][:, block(j)], ident_f32[:])
-            masked[group, tile_j] = bank
+                nc.tensor.transpose(bank[:, j, :], flipped[pair, t][:, block(j)], ident_f32[:])
+            held[pair, t] = bank
 
-        def copy_shared(group):
-            direct[group] = flow.tile([P, PACK, SPARE + P], F32, name="direct", tag="direct", bufs=2)
-            nc.scalar.copy(out=direct[group][:, :, :SPARE], in_=masked[group, HELD - 1][:, :, P - SPARE:])
-
-        w_bf, state_bank = {}, {}
+        def copy_shared(pair):
+            in_sbuf[pair] = flow.tile([P, PACK, SPARE + P], F32, name="in_sbuf", tag="in_sbuf", bufs=2)
+            nc.scalar.copy(out=in_sbuf[pair][:, :, :SPARE], in_=held[pair, SHARED_TILE][:, :, P - SPARE:])
 
         def scale_values(h, engine):
             tag = "w_first" if h < 2 else "w%d" % h
             w_bf[h] = flow.tile([P, GROUPS, W * PACK], BF16, name="w_bf", tag=tag, bufs=1, align_bytes=64)
             for g in range(GROUPS):
-                hg = h * GROUPS + g
+                step_size = dt_first[:, g, :] if h == 0 else dt_rest[:, (h - 1) * GROUPS + g, :]
+                target = packed_view(w_bf[h][:, g, :])
                 engine.tensor_tensor(
-                    out=packed_view(w_bf[h][:, g, :]),
+                    out=target,
                     in0=rows_view(v_raw[h][:, g, :].rearrange("p (j w) -> p j w", j=PACK)),
-                    in1=dt_col[:, hg, :].unsqueeze(1).unsqueeze(3).to_broadcast([P, W // RUN, PACK, RUN]),
+                    in1=step_size.unsqueeze(1).unsqueeze(3).to_broadcast(target.shape),
                     op=ALU.mult)
 
         def quantize_values(h):
-            quantize(wq[h][0][:], wq[h][1][:], w_bf[h][:].rearrange("p g x -> p (g x)"))
+            quantize(wq[h], block(0, GROUPS * W), w_bf[h][:].rearrange("p g x -> p (g x)"))
 
         def pack_state():
-            h0_bf = keep.tile([P, H, W * PACK], BF16, align_bytes=64)
+            packed = keep.tile([P, H, W * PACK], BF16, name="h0_packed", align_bytes=64)
             for h in range(H):
-                nc.scalar.copy(out=packed_view(h0_bf[:, h, :]),
+                nc.scalar.copy(out=packed_view(packed[:, h, :]),
                                in_=rows_view(h0_raw[:, h, :].rearrange("p (j w) -> p j w", j=PACK)))
-            return h0_bf
+            return packed
 
-        def read_state(tg, j):
-            bank = psum.tile([P, H * W], F32, tag="inner", bufs=BANKS["inner"])
-            multiply(bank[:], cq[tg], block(j), hq, slice(0, H * W), True, True)
-            state_bank[tg, j] = bank
+        def read_state(i):
+            g, j = divmod(i, PACK)
+            state_bank[i] = bank_tile([P, H * W], F32, "inner")
+            multiply(state_bank[i][:], cq[g], block(j), hq, block(0, H * W))
 
-        def copy_state(tg, j):
-            nc.scalar.copy(out=read[tg][:, j, :], in_=state_bank[tg, j][:])
-
-        def step_of(k):
-            return k // (H * GROUPS), (k // H) % GROUPS, k % H
-
-        decay, m_bf, mq, inner, result, result_bf = {}, {}, {}, {}, {}, {}
+        def copy_state(i):
+            g, j = divmod(i, PACK)
+            nc.scalar.copy(out=state_read[g][:, j, :], in_=state_bank[i][:])
 
         def decays(k):
-            tg, g, h = step_of(k)
-            decay[k] = flow.tile([P, PACK, GROUP], F32, name="decay", tag="decay", bufs=CFG["lead"] + 2)
+            target_group, source_group, h = step_of(k)
+            decay[k] = flow.tile([P, PACK, GROUP], F32, name="decay", tag="decay", bufs=DECAY_LEAD + 2)
             for j in range(PACK):
-                i = g * PACK + j
-                nc.scalar.activation(out=decay[k][:, j, :], in_=later[:, i, block(tg, GROUP)], func=ACT.Exp,
+                i = source_group * PACK + j
+                nc.scalar.activation(out=decay[k][:, j, :], in_=later[:, i, block(target_group, GROUP)], func=ACT.Exp,
                                      scale=neg_lam[:, h:h + 1], bias=lam_age[:, h, i:i + 1])
 
         def decay_scores(k):
-            group = k // H
-            low = flow.tile([P, 2 * P * PACK], BF16, name="m_low", tag="m_low", bufs=2, align_bytes=64)
-            high = flow.tile([P, 2 * P * PACK], BF16, name="m_high", tag="m_high", bufs=2, align_bytes=64)
+            pair = k // H
+            low = flow.tile([P, 2 * GROUP], BF16, name="m_low", tag="m_low", bufs=2, align_bytes=64)
+            high = flow.tile([P, 2 * GROUP], BF16, name="m_high", tag="m_high", bufs=2, align_bytes=64)
             m_bf[k] = (low, high)
-            split = P - SHARE[k]
+            share = share_of(k)
+            split = P - share
             nc.gpsimd.tensor_tensor(out=packed_view(high[:, split * PACK:]),
-                                    in0=rows_view(direct[group][:, :, SPARE - SHARE[k]:]),
-                                    in1=rows_view(decay[k][:, :, 2 * P + split:]), op=ALU.mult)
-            for tile_j in ORDER:
-                width = split if tile_j == HELD - 1 else P
-                target = high[:, :split * PACK] if tile_j == HELD - 1 else low[:, block(tile_j, P * PACK)]
-                nc.vector.tensor_tensor(out=packed_view(target, 2), in0=rows_view(masked[group, tile_j][:, :, :width], 2),
-                                        in1=rows_view(decay[k][:, :, tile_j * P:tile_j * P + width], 2), op=ALU.mult)
+                                    in0=rows_view(in_sbuf[pair][:, :, SPARE - share:]),
+                                    in1=rows_view(decay[k][:, :, SHARED_TILE * P + split:]), op=ALU.mult)
+            for t in HELD_ORDER:
+                width = split if t == SHARED_TILE else P
+                target = high[:, :split * PACK] if t == SHARED_TILE else low[:, block(t, GROUP)]
+                nc.vector.tensor_tensor(out=packed_view(target, 2), in0=rows_view(held[pair, t][:, :, :width], 2),
+                                        in1=rows_view(decay[k][:, :, t * P:t * P + width], 2), op=ALU.mult)
 
         def quantize_scores(k):
-            tg, g, h = step_of(k)
-            codes = flow.tile([P, GROUP], U32, name="m_codes", tag="m_codes", bufs=6, align_bytes=64)
-            scales = flow.tile([P, GROUP], U8, name="m_scales", tag="m_scales", bufs=6, align_bytes=64)
+            codes = flow.tile([P, GROUP], U32, name="m_codes", tag="m_codes", bufs=H + 2, align_bytes=64)
+            scales = flow.tile([P, GROUP], U8, name="m_scales", tag="m_scales", bufs=H + 2, align_bytes=64)
             mq[k] = (codes, scales)
             for half in (1, 0):
-                quantize(codes[:, block(half, 2 * P)], scales[:, block(half, 2 * P)], m_bf[k][half][:])
-            if g == GROUPS - 1:
-                u = tg * H + h
-                tag = "score" if u == GROUPS * H - 1 else "inner"
-                inner[u] = psum.tile([P, PACK, W], F32, name="inner", tag=tag, bufs=BANKS[tag])
-                for j in range(PACK):
-                    for gg in range(GROUPS):
-                        multiply(inner[u][:, j, :], mq[k - (GROUPS - 1 - gg) * H], block(j), wq[h], block(gg), gg == 0,
-                                 gg == GROUPS - 1)
+                quantize(mq[k], block(half, 2 * P), m_bf[k][half][:])
+            unit = unit_closed_by(k)
+            if unit is not None:
+                inner[unit] = bank_tile([P, PACK, W], F32, "score" if unit == UNITS - 1 else "inner")
+                for t in range(PACK):
+                    for g in range(GROUPS):
+                        multiply(inner[unit][:, t, :], mq[k - (GROUPS - 1 - g) * H], block(t), wq[unit % H], block(g),
+                                 start=g == 0, stop=g == GROUPS - 1)
 
-        def finish(u):
-            tg, h = divmod(u, H)
-            result[u] = flow.tile([P, PACK, W], F32, name="result", tag="result", bufs=8)
-            for j in range(PACK):
-                k = tg * PACK + j
-                nc.vector.scalar_tensor_tensor(out=result[u][:, j, :], in0=read[tg][:, j, block(h)],
-                                               scalar=carry[:, h, k:k + 1], in1=inner[u][:, j, :],
+        def finish(unit):
+            g, h = divmod(unit, H)
+            result[unit] = flow.tile([P, PACK, W], F32, name="result", tag="result", bufs=UNITS)
+            for t in range(PACK):
+                i = g * PACK + t
+                nc.vector.scalar_tensor_tensor(out=result[unit][:, t, :], in0=state_read[g][:, t, block(h)],
+                                               scalar=carry[:, h, i:i + 1], in1=inner[unit][:, t, :],
                                                op0=ALU.mult, op1=ALU.add)
-            nc.sync.dma_start(out=out_0[0, h, block(tg, GROUP), :].rearrange("(p j) w -> p j w", j=PACK),
-                              in_=result[u][:])
+            nc.sync.dma_start(out=out_0[0, h, block(g, GROUP), :].rearrange("(p t) w -> p t w", t=PACK),
+                              in_=result[unit][:])
 
-        def round_result(u, copy):
-            result_bf[u] = flow.tile([P, W * PACK], BF16, name="result_bf", tag="result_bf", bufs=6, align_bytes=64)
-            copy(out=packed_view(result_bf[u][:]), in_=rows_view(result[u][:]))
+        def round_result(unit, copy):
+            result_bf[unit] = flow.tile([P, W * PACK], BF16, name="result_bf", tag="result_bf", bufs=6, align_bytes=64)
+            copy(out=packed_view(result_bf[unit][:]), in_=rows_view(result[unit][:]))
 
-        def quantize_result(u):
-            tg, h = divmod(u, H)
-            codes, scales = oq[tg]
-            quantize(codes[:, block(h)], scales[:, block(h)], result_bf[u][:])
-            nc.sync.dma_start(out=out_1[tg].rearrange("p m t -> p (m t)").bitcast(I32)[:, block(h)],
+        def quantize_result(unit):
+            g, h = divmod(unit, H)
+            codes, scales = planes[g]
+            quantize(planes[g], block(h), result_bf[unit][:])
+            nc.sync.dma_start(out=out_1[g].rearrange("p m t -> p (m t)").bitcast(I32)[:, block(h)],
                               in_=codes[:, block(h)].bitcast(I32))
             if h == H - 1:
                 for q in range(4):
-                    queue = nc.scalar if q % 2 == 0 and tg == GROUPS - 1 else nc.sync
-                    queue.dma_start(out=out_2[tg, 4 * q:4 * q + 4, :].bitcast(I32),
+                    queue = nc.scalar if q % 2 == 0 and g == GROUPS - 1 else nc.sync
+                    queue.dma_start(out=out_2[g, 4 * q:4 * q + 4, :].bitcast(I32),
                                     in_=scales[32 * q:32 * q + 4, :].bitcast(I32))
 
-        cm_turned = turn(cm_raw[0], "held")
-        bm_turned = turn(bm_raw[0], "held")
-        quantize(cq[0][0][:], cq[0][1][:], cm_turned[:])
-        quantize(bq[0][0][:], bq[0][1][:], bm_turned[:])
+        for i in range(TILES):
+            nc.vector.tensor_scalar(out=later[:, i, :], in0=age_row[:], scalar1=age_tiles[:, i:i + 1], scalar2=None,
+                                    op0=ALU.max)
+
+        bm_turned = pack_rows(transpose_rows(bm_raw[0], "held"))
+        cm_turned = pack_rows(transpose_rows(cm_raw[0], "held", (1, 0)))
+        quantize(bq[0], block(0, GROUP), bm_turned[:])
+        for half in (1, 0):
+            quantize(cq[0], block(half, 2 * P), cm_turned[:, block(half, 2 * GROUP)])
         scale_values(0, nc.vector)
-        if not CFG["bm1first"]:
-            decays(0)
-        bm_later = turn(bm_raw[1], "held")
-        if CFG["bm1first"]:
-            decays(0)
-        tiles = ORDER + (HELD,)
-        for tile_j, tag in zip(tiles, ("score", "inner", "inner", "held")):
-            scores(0, tile_j, tag)
-        for tile_j in ORDER[:2]:
-            mask_scores(0, tile_j)
-            hold_scores(0, tile_j)
+        bm_banks = transpose_rows(bm_raw[1], "held")
+        for t, tag in zip(HELD_ORDER, ("score", "inner", "inner")):
+            scores(0, t, tag)
+        bm_turned = pack_rows(bm_banks)
+        decays(0)
+        scores(0, SBUF_TILE, "held")
+        for t in HELD_ORDER[:2]:
+            mask_scores(0, t)
+            hold_scores(0, t)
         copy_shared(0)
         decays(1)
-        quantize(bq[1][0][:], bq[1][1][:], bm_later[:])
+        quantize(bq[1], block(0, GROUP), bm_turned[:])
         quantize_values(0)
-        if CFG["w1g"]:
-            scale_values(1, nc.gpsimd)
-        mask_scores(0, ORDER[2])
-        hold_scores(0, ORDER[2])
-        mask_scores(0, HELD)
-        for k in range(2, CFG["lead"]):
+        scale_values(1, nc.gpsimd)
+        mask_scores(0, HELD_ORDER[2])
+        hold_scores(0, HELD_ORDER[2])
+        mask_scores(0, SBUF_TILE)
+        for k in range(2, DECAY_LEAD):
             decays(k)
 
-        steps = GROUPS * GROUPS * H
-
-        def unit_at(k, lag):
-            tg, g, h = step_of(max(k - lag, 0))
-            return tg * H + h if k >= lag and g == GROUPS - 1 else None
-
-        for k in range(steps):
-            tg, g, h = step_of(k)
-            ahead = k // H + 1
-            more = ahead < GROUPS * GROUPS
-            if more:
-                scores(ahead, tiles[h], "score")
-            for i in range(8):
-                if CFG["read"][i] == k:
-                    read_state(i // 4, i % 4)
-            if k == CFG["cm1"]:
-                cm_banks = turn_a(cm_raw[1], "inner")
+        for k in range(STEPS - 1):
+            h = k % H
+            next_pair = k // H + 1
+            has_next = next_pair < GROUPS * GROUPS
+            state_tiles = [i for i in range(TILES) if READ_STATE_STEPS[i] == k]
+            if has_next:
+                scores(next_pair, TILE_ORDER[h], "score")
+            for i in state_tiles:
+                read_state(i)
+            if k == TURN_CM_STEP:
+                cm_banks = transpose_rows(cm_raw[1], "inner")
             decay_scores(k)
-            if k == steps - 1:
-                break
-            if more and h == H - 1:
-                hold_scores(ahead, ORDER[-1])
-            if k == CFG["cm1"]:
-                cm_turned = turn_b(cm_banks)
-            for i in range(8):
-                if CFG["read"][i] == k:
-                    copy_state(i // 4, i % 4)
-            for u in range(5):
-                if CFG["round"][u] == k and CFG["early"] and u < 4:
-                    round_result(u, nc.scalar.copy)
-            if k + CFG["lead"] < steps:
-                decays(k + CFG["lead"])
-            if k == CFG["pack"]:
-                h0_bf = pack_state()
-            if unit_at(k, 2) is not None:
-                finish(unit_at(k, 2))
-            for u in range(5):
-                if CFG["round"][u] == k and (u == 4 or not CFG["early"]):
-                    round_result(u, nc.scalar.copy)
-            if more:
-                if h == CFG["shared"]:
-                    copy_shared(ahead)
-                mask_scores(ahead, tiles[h])
-                if h < HELD - 1:
-                    hold_scores(ahead, tiles[h])
-            for hh in range(1, H):
-                if CFG["wq"][hh] == k:
-                    quantize_values(hh)
-            for hh in range(1, H):
-                if CFG["w"][hh] == k and not (hh == 1 and CFG["w1g"]):
-                    scale_values(hh, nc.vector)
-            if k == CFG["hq"]:
-                quantize(hq[0][:], hq[1][:], h0_bf[:].rearrange("p h x -> p (h x)"))
-            if k == CFG["cq1"]:
-                quantize(cq[1][0][:], cq[1][1][:], cm_turned[:])
-            for u in range(4):
-                if CFG["q"][u] == k:
-                    quantize_result(u)
+            if has_next and h == H - 1:
+                hold_scores(next_pair, HELD_ORDER[2])
+            if k == TURN_CM_STEP:
+                cm_turned = pack_rows(cm_banks)
+            for i in state_tiles:
+                copy_state(i)
+            if k + DECAY_LEAD < STEPS:
+                decays(k + DECAY_LEAD)
+            if k == PACK_STATE_STEP:
+                h0_packed = pack_state()
+            unit = unit_closed_by(k - FINISH_LAG)
+            if unit is not None:
+                finish(unit)
+                round_result(unit, nc.scalar.copy)
+            if has_next:
+                if h == 1:
+                    copy_shared(next_pair)
+                mask_scores(next_pair, TILE_ORDER[h])
+                if h < 2:
+                    hold_scores(next_pair, TILE_ORDER[h])
+            if 2 <= k <= H:
+                quantize_values(k - 1)
+            if 2 <= k < H:
+                scale_values(k, nc.vector)
+            if k == QUANTIZE_STATE_STEP:
+                quantize(hq, block(0, H * W), h0_packed[:].rearrange("p h x -> p (h x)"))
+            if k == QUANTIZE_CM_STEP:
+                quantize(cq[1], block(0, GROUP), cm_turned[:])
+            unit = unit_closed_by(k - PLANES_LAG)
+            if unit is not None:
+                quantize_result(unit)
             if k >= 1:
                 quantize_scores(k - 1)
-        last = GROUPS * H - 1
-        quantize_scores(steps - 2)
-        quantize_scores(steps - 1)
-        finish(last - 2)
-        round_result(last - 2, nc.scalar.copy)
-        finish(last - 1)
-        round_result(last - 1, nc.scalar.copy)
+
+        last = UNITS - 1
+        decay_scores(STEPS - 1)
+        quantize_scores(STEPS - 2)
+        quantize_scores(STEPS - 1)
+        for unit in (last - 2, last - 1):
+            finish(unit)
+            round_result(unit, nc.scalar.copy)
         quantize_result(last - 3)
         finish(last)
         quantize_result(last - 2)

from contextlib import ExitStack

import concourse.mybir as mybir
from concourse.masks import make_identity

S, H, W, N = 1024, 4, 128, 512
FLOPS = 2 * S * S * N + 2 * H * S * S * W + 2 * H * S * N * W

F32 = mybir.dt.float32
BF16 = mybir.dt.bfloat16
U32 = mybir.dt.uint32
I32 = mybir.dt.int32
U8 = mybir.dt.uint8
FP8X4 = mybir.dt.float8_e4m3fn_x4
ALU = mybir.AluOpType
ACT = mybir.ActivationFunctionType

P = 128
PACK = 4
GROUP = P * PACK
GROUPS = S // GROUP
TILES = GROUPS * PACK
STEPS = GROUPS * GROUPS * H
UNITS = GROUPS * H

SHARED_TILE, SBUF_TILE = 2, 3
HELD_ORDER = (SHARED_TILE, 0, 1)
TILE_ORDER = HELD_ORDER + (SBUF_TILE,)

SHARE_BY_READERS = (8, 56, 96)
SPARE = max(SHARE_BY_READERS)

BANKS = {"held": 5, "score": 1, "inner": 2}

DECAY_LEAD = 3
FINISH_LAG = 2
PLANES_LAG = 4

PACK_STATE_STEP, TURN_CM_STEP, QUANTIZE_STATE_STEP, QUANTIZE_CM_STEP = 0, 2, 2, 3
READ_STATE_STEPS = (3, 3, 4, 4, 10, 10, 11, 12)


def step_of(k):
    return k // (H * GROUPS), (k // H) % GROUPS, k % H


def unit_closed_by(k):
    if k < 0:
        return None
    target_group, source_group, head = step_of(k)
    return target_group * H + head if source_group == GROUPS - 1 else None


def share_of(k):
    if k < 2:
        return 0
    has_mask = k < STEPS - H
    has_sum = unit_closed_by(k - FINISH_LAG) is not None and k < STEPS - 1
    return SHARE_BY_READERS[int(has_mask) + int(has_sum)]


def block(i, width=P):
    return slice(i * width, (i + 1) * width)


def rows_view(ap, run=4):
    return ap.rearrange("p j (c i) -> p c j i", i=run)


def packed_view(ap, run=4):
    return ap.rearrange("p (c i j) -> p c j i", i=run, j=PACK)


def tile_eventtimestatespacedualchunk_x1_kernel(tc, cm, bm, v, dt, age, lam, h0, out_0, out_1, out_2):
    nc = tc.nc
    with ExitStack() as ctx:
        keep = ctx.enter_context(tc.tile_pool(name="keep", bufs=1))
        flow = ctx.enter_context(tc.tile_pool(name="flow", bufs=2))
        psum = ctx.enter_context(tc.psum_pool(name="psum", bufs=2))
        ctx.enter_context(tc.manual_schedule())

        def bank_tile(shape, dtype, tag):
            return psum.tile(shape, dtype, name=tag, tag=tag, bufs=BANKS[tag])

        def operand(name, width):
            codes = keep.tile([P, width], U32, name=name + "_codes", align_bytes=64)
            scales = keep.tile([P, width], U8, name=name + "_scales", align_bytes=64)
            return codes, scales

        def quantize(target, cols, values):
            codes, scales = target
            nc.vector.quantize_mx(out=codes[:, cols].bitcast(FP8X4), scales=scales[:, cols], in_=values)

        def multiply(acc, lhs, lhs_cols, rhs, rhs_cols, start=True, stop=True):
            nc.tensor.matmul_mx(
                out=acc,
                lhsT=lhs[0][:, lhs_cols].bitcast(FP8X4), lhsT_scale=lhs[1][:, lhs_cols],
                rhs=rhs[0][:, rhs_cols].bitcast(FP8X4), rhs_scale=rhs[1][:, rhs_cols],
                start=start, stop=stop,
            )

        def load_rows(name, x, g):
            raw = keep.tile([P, PACK, N], BF16, name=name)
            nc.sync.dma_start(out=raw[:], in_=x[0, block(g, GROUP), :].rearrange("(p j) n -> p j n", j=PACK))
            return raw

        def load_values(h):
            raw = keep.tile([P, GROUPS, PACK * W], BF16, name="v_raw%d" % h)
            nc.sync.dma_start(out=raw[:], in_=v[0, h].rearrange("(g p j) w -> p g (j w)", p=P, j=PACK))
            return raw

        age_col = keep.tile([P, GROUPS, PACK], BF16)
        nc.sync.dma_start(out=age_col[:], in_=age[0].rearrange("(g p j) -> p g j", p=P, j=PACK))
        lam_all = keep.tile([P, H], BF16)
        nc.sync.dma_start(out=lam_all[:], in_=lam.partition_broadcast(P))
        bm_raw = [load_rows("bm_raw0", bm, 0)]
        cm_raw = [load_rows("cm_raw0", cm, 0)]
        bm_raw.append(load_rows("bm_raw1", bm, 1))
        dt_first = keep.tile([P, GROUPS, PACK], BF16)
        nc.sync.dma_start(out=dt_first[:], in_=dt[0, 0].rearrange("(g p j) -> p g j", p=P, j=PACK))
        v_raw = [load_values(0)]
        dt_rest = keep.tile([P, (H - 1) * GROUPS, PACK], BF16)
        nc.sync.dma_start(out=dt_rest[:], in_=dt[0, 1:].rearrange("h (g p j) -> p (h g) j", p=P, j=PACK))
        v_raw.append(load_values(1))
        h0_raw = keep.tile([P, H, PACK * W], BF16)
        nc.sync.dma_start(out=h0_raw[:], in_=h0[0].rearrange("h (p j) w -> p h (j w)", j=PACK))
        cm_raw.append(load_rows("cm_raw1", cm, 1))
        for h in range(2, H):
            v_raw.append(load_values(h))

        ident_bf = keep.tile([P, P], BF16)
        make_identity(nc, ident_bf[:])
        ident_f32 = keep.tile([P, P], F32)
        make_identity(nc, ident_f32[:])

        age_tiles = age_col[:].rearrange("p g j -> p (g j)")
        lam_age = keep.tile([P, H, TILES], F32)
        nc.vector.tensor_tensor(
            out=lam_age[:],
            in0=age_tiles.unsqueeze(1).to_broadcast([P, H, TILES]),
            in1=lam_all[:].unsqueeze(2).to_broadcast([P, H, TILES]),
            op=ALU.mult,
        )
        neg_lam = keep.tile([P, H], F32)
        nc.vector.tensor_scalar(out=neg_lam[:], in0=lam_all[:], scalar1=-1.0, scalar2=None, op0=ALU.mult)
        carry = keep.tile([P, H, TILES], F32)
        nc.scalar.activation(out=carry[:], in_=lam_age[:], func=ACT.Exp, scale=-1.0)

        spread = bank_tile([P, S], BF16, "held")
        for i in range(TILES):
            nc.tensor.matmul(spread[:, block(i)], lhsT=age_tiles[:, i:i + 1].to_broadcast([P, P]), rhs=ident_bf[:],
                             start=True, stop=True)
        age_row = keep.tile([P, S], BF16)
        nc.vector.tensor_copy(out=age_row[:], in_=spread[:])

        cq = [operand("cq%d" % g, GROUP) for g in range(GROUPS)]
        bq = [operand("bq%d" % g, GROUP) for g in range(GROUPS)]
        wq = [operand("wq%d" % h, GROUPS * W) for h in range(H)]
        hq = operand("hq", H * W)
        planes = [operand("planes%d" % g, H * W) for g in range(GROUPS)]
        later = keep.tile([P, TILES, S], BF16)
        state_read = [keep.tile([P, PACK, H * W], F32, name="state_read%d" % g) for g in range(GROUPS)]
        score, flipped, held, in_sbuf, state_bank = {}, {}, {}, {}, {}
        w_bf, decay, m_bf, mq, inner, result, result_bf = {}, {}, {}, {}, {}, {}, {}

        def transpose_rows(raw, tag, bank_order=(0, 1)):
            words = raw[:].rearrange("p j n -> p (j n)").bitcast(F32)
            row_words = N // 2
            banks = {}
            for b in bank_order:
                bank = bank_tile([P, 2, 2, P], F32, tag)
                for jj in range(2):
                    j = 2 * b + jj
                    for u in range(2):
                        nc.tensor.transpose(bank[:, jj, u, :], words[:, row_words * j + u:row_words * (j + 1):2],
                                            ident_f32[:])
                banks[b] = bank
            return banks

        def pack_rows(banks):
            turned = flow.tile([P, GROUP * PACK], BF16, tag="turned", bufs=3, align_bytes=64)
            turned_words = turned[:].bitcast(F32)
            for b in banks:
                nc.scalar.copy(out=turned_words[:, block(b, GROUP)].rearrange("p (jj m u) -> p jj m u", jj=2, u=2),
                               in_=banks[b][:].rearrange("p jj u m -> p jj m u"))
            return turned

        def scores(pair, t, tag):
            target_group, source_group = divmod(pair, GROUPS)
            bank = bank_tile([P, PACK, P], F32, tag)
            score[pair, t] = bank
            if t == SBUF_TILE:
                for j in range(PACK):
                    multiply(bank[:, j, :], bq[source_group], block(j), cq[target_group], block(t))
            else:
                multiply(bank[:].rearrange("p j m -> p (j m)"), cq[target_group], block(t), bq[source_group],
                         block(0, GROUP))

        def mask_scores(pair, t):
            target_group, source_group = divmod(pair, GROUPS)
            bank = score[pair, t]
            target_tile = target_group * PACK + t
            if t == SBUF_TILE:
                for j in range(PACK):
                    i = source_group * PACK + j
                    nc.vector.scalar_tensor_tensor(
                        out=in_sbuf[pair][:, j, SPARE:], in0=age_row[:, block(target_tile)],
                        scalar=age_tiles[:, i:i + 1], in1=bank[:, j, :], op0=ALU.is_ge, op1=ALU.mult)
            else:
                flipped[pair, t] = flow.tile([P, GROUP], F32, name="flipped", tag="flipped", bufs=3)
                nc.vector.scalar_tensor_tensor(
                    out=flipped[pair, t][:], in0=age_row[:, block(source_group, GROUP)],
                    scalar=age_tiles[:, target_tile:target_tile + 1], in1=bank[:].rearrange("p j m -> p (j m)"),
                    op0=ALU.is_le, op1=ALU.mult)

        def hold_scores(pair, t):
            bank = bank_tile([P, PACK, P], F32, "held")
            for j in range(PACK):
                nc.tensor.transpose(bank[:, j, :], flipped[pair, t][:, block(j)], ident_f32[:])
            held[pair, t] = bank

        def copy_shared(pair):
            in_sbuf[pair] = flow.tile([P, PACK, SPARE + P], F32, name="in_sbuf", tag="in_sbuf", bufs=2)
            nc.scalar.copy(out=in_sbuf[pair][:, :, :SPARE], in_=held[pair, SHARED_TILE][:, :, P - SPARE:])

        def scale_values(h, engine):
            tag = "w_first" if h < 2 else "w%d" % h
            w_bf[h] = flow.tile([P, GROUPS, W * PACK], BF16, name="w_bf", tag=tag, bufs=1, align_bytes=64)
            for g in range(GROUPS):
                step_size = dt_first[:, g, :] if h == 0 else dt_rest[:, (h - 1) * GROUPS + g, :]
                target = packed_view(w_bf[h][:, g, :])
                engine.tensor_tensor(
                    out=target,
                    in0=rows_view(v_raw[h][:, g, :].rearrange("p (j w) -> p j w", j=PACK)),
                    in1=step_size.unsqueeze(1).unsqueeze(3).to_broadcast(target.shape),
                    op=ALU.mult)

        def quantize_values(h):
            quantize(wq[h], block(0, GROUPS * W), w_bf[h][:].rearrange("p g x -> p (g x)"))

        def pack_state():
            packed = keep.tile([P, H, W * PACK], BF16, name="h0_packed", align_bytes=64)
            for h in range(H):
                nc.scalar.copy(out=packed_view(packed[:, h, :]),
                               in_=rows_view(h0_raw[:, h, :].rearrange("p (j w) -> p j w", j=PACK)))
            return packed

        def read_state(i):
            g, j = divmod(i, PACK)
            state_bank[i] = bank_tile([P, H * W], F32, "inner")
            multiply(state_bank[i][:], cq[g], block(j), hq, block(0, H * W))

        def copy_state(i):
            g, j = divmod(i, PACK)
            nc.scalar.copy(out=state_read[g][:, j, :], in_=state_bank[i][:])

        def decays(k):
            target_group, source_group, h = step_of(k)
            decay[k] = flow.tile([P, PACK, GROUP], F32, name="decay", tag="decay", bufs=DECAY_LEAD + 2)
            for j in range(PACK):
                i = source_group * PACK + j
                nc.scalar.activation(out=decay[k][:, j, :], in_=later[:, i, block(target_group, GROUP)], func=ACT.Exp,
                                     scale=neg_lam[:, h:h + 1], bias=lam_age[:, h, i:i + 1])

        def decay_scores(k):
            pair = k // H
            low = flow.tile([P, 2 * GROUP], BF16, name="m_low", tag="m_low", bufs=2, align_bytes=64)
            high = flow.tile([P, 2 * GROUP], BF16, name="m_high", tag="m_high", bufs=2, align_bytes=64)
            m_bf[k] = (low, high)
            share = share_of(k)
            split = P - share
            nc.gpsimd.tensor_tensor(out=packed_view(high[:, split * PACK:]),
                                    in0=rows_view(in_sbuf[pair][:, :, SPARE - share:]),
                                    in1=rows_view(decay[k][:, :, SHARED_TILE * P + split:]), op=ALU.mult)
            for t in HELD_ORDER:
                width = split if t == SHARED_TILE else P
                target = high[:, :split * PACK] if t == SHARED_TILE else low[:, block(t, GROUP)]
                nc.vector.tensor_tensor(out=packed_view(target, 2), in0=rows_view(held[pair, t][:, :, :width], 2),
                                        in1=rows_view(decay[k][:, :, t * P:t * P + width], 2), op=ALU.mult)

        def quantize_scores(k):
            codes = flow.tile([P, GROUP], U32, name="m_codes", tag="m_codes", bufs=H + 2, align_bytes=64)
            scales = flow.tile([P, GROUP], U8, name="m_scales", tag="m_scales", bufs=H + 2, align_bytes=64)
            mq[k] = (codes, scales)
            for half in (1, 0):
                quantize(mq[k], block(half, 2 * P), m_bf[k][half][:])
            unit = unit_closed_by(k)
            if unit is not None:
                inner[unit] = bank_tile([P, PACK, W], F32, "score" if unit == UNITS - 1 else "inner")
                for t in range(PACK):
                    for g in range(GROUPS):
                        multiply(inner[unit][:, t, :], mq[k - (GROUPS - 1 - g) * H], block(t), wq[unit % H], block(g),
                                 start=g == 0, stop=g == GROUPS - 1)

        def finish(unit):
            g, h = divmod(unit, H)
            result[unit] = flow.tile([P, PACK, W], F32, name="result", tag="result", bufs=UNITS)
            for t in range(PACK):
                i = g * PACK + t
                nc.vector.scalar_tensor_tensor(out=result[unit][:, t, :], in0=state_read[g][:, t, block(h)],
                                               scalar=carry[:, h, i:i + 1], in1=inner[unit][:, t, :],
                                               op0=ALU.mult, op1=ALU.add)
            nc.sync.dma_start(out=out_0[0, h, block(g, GROUP), :].rearrange("(p t) w -> p t w", t=PACK),
                              in_=result[unit][:])

        def round_result(unit, copy):
            result_bf[unit] = flow.tile([P, W * PACK], BF16, name="result_bf", tag="result_bf", bufs=6, align_bytes=64)
            copy(out=packed_view(result_bf[unit][:]), in_=rows_view(result[unit][:]))

        def quantize_result(unit):
            g, h = divmod(unit, H)
            codes, scales = planes[g]
            quantize(planes[g], block(h), result_bf[unit][:])
            nc.sync.dma_start(out=out_1[g].rearrange("p m t -> p (m t)").bitcast(I32)[:, block(h)],
                              in_=codes[:, block(h)].bitcast(I32))
            if h == H - 1:
                for q in range(4):
                    queue = nc.scalar if q % 2 == 0 and g == GROUPS - 1 else nc.sync
                    queue.dma_start(out=out_2[g, 4 * q:4 * q + 4, :].bitcast(I32),
                                    in_=scales[32 * q:32 * q + 4, :].bitcast(I32))

        for i in range(TILES):
            nc.vector.tensor_scalar(out=later[:, i, :], in0=age_row[:], scalar1=age_tiles[:, i:i + 1], scalar2=None,
                                    op0=ALU.max)

        bm_turned = pack_rows(transpose_rows(bm_raw[0], "held"))
        cm_turned = pack_rows(transpose_rows(cm_raw[0], "held", (1, 0)))
        quantize(bq[0], block(0, GROUP), bm_turned[:])
        for half in (1, 0):
            quantize(cq[0], block(half, 2 * P), cm_turned[:, block(half, 2 * GROUP)])
        scale_values(0, nc.vector)
        bm_banks = transpose_rows(bm_raw[1], "held")
        for t, tag in zip(HELD_ORDER, ("score", "inner", "inner")):
            scores(0, t, tag)
        bm_turned = pack_rows(bm_banks)
        decays(0)
        scores(0, SBUF_TILE, "held")
        for t in HELD_ORDER[:2]:
            mask_scores(0, t)
            hold_scores(0, t)
        copy_shared(0)
        decays(1)
        quantize(bq[1], block(0, GROUP), bm_turned[:])
        quantize_values(0)
        scale_values(1, nc.gpsimd)
        mask_scores(0, HELD_ORDER[2])
        hold_scores(0, HELD_ORDER[2])
        mask_scores(0, SBUF_TILE)
        for k in range(2, DECAY_LEAD):
            decays(k)

        for k in range(STEPS - 1):
            h = k % H
            next_pair = k // H + 1
            has_next = next_pair < GROUPS * GROUPS
            state_tiles = [i for i in range(TILES) if READ_STATE_STEPS[i] == k]
            if has_next:
                scores(next_pair, TILE_ORDER[h], "score")
            for i in state_tiles:
                read_state(i)
            if k == TURN_CM_STEP:
                cm_banks = transpose_rows(cm_raw[1], "inner")
            decay_scores(k)
            if has_next and h == H - 1:
                hold_scores(next_pair, HELD_ORDER[2])
            if k == TURN_CM_STEP:
                cm_turned = pack_rows(cm_banks)
            for i in state_tiles:
                copy_state(i)
            if k + DECAY_LEAD < STEPS:
                decays(k + DECAY_LEAD)
            if k == PACK_STATE_STEP:
                h0_packed = pack_state()
            unit = unit_closed_by(k - FINISH_LAG)
            if unit is not None:
                finish(unit)
                round_result(unit, nc.scalar.copy)
            if has_next:
                if h == 1:
                    copy_shared(next_pair)
                mask_scores(next_pair, TILE_ORDER[h])
                if h < 2:
                    hold_scores(next_pair, TILE_ORDER[h])
            if 2 <= k <= H:
                quantize_values(k - 1)
            if 2 <= k < H:
                scale_values(k, nc.vector)
            if k == QUANTIZE_STATE_STEP:
                quantize(hq, block(0, H * W), h0_packed[:].rearrange("p h x -> p (h x)"))
            if k == QUANTIZE_CM_STEP:
                quantize(cq[1], block(0, GROUP), cm_turned[:])
            unit = unit_closed_by(k - PLANES_LAG)
            if unit is not None:
                quantize_result(unit)
            if k >= 1:
                quantize_scores(k - 1)

        last = UNITS - 1
        decay_scores(STEPS - 1)
        quantize_scores(STEPS - 2)
        quantize_scores(STEPS - 1)
        for unit in (last - 2, last - 1):
            finish(unit)
            round_result(unit, nc.scalar.copy)
        quantize_result(last - 3)
        finish(last)
        quantize_result(last - 2)
        round_result(last, nc.vector.tensor_copy)
        quantize_result(last - 1)
        quantize_result(last)
